import numpy as np
import ml_dtypes


def mxq(x, axis, fmt="e4m3"):
    dtype, down = {"e4m3": (ml_dtypes.float8_e4m3fn, 7), "e5m2": (ml_dtypes.float8_e5m2, 14)}[fmt]
    v = np.moveaxis(np.asarray(x, np.float32).astype(ml_dtypes.bfloat16).astype(np.float64), axis, -1)
    blocks = v.reshape(v.shape[:-1] + (-1, 32))
    amax = np.abs(blocks).max(-1, keepdims=True)
    byte = np.maximum(np.where(amax > 0, np.frexp(amax)[1] - 1 + 127, 0) - down, 1)
    scale = np.exp2(byte - 127.0)
    codes = (blocks / scale).astype(np.float32).astype(dtype).astype(np.float64)
    return np.moveaxis((codes * scale).reshape(v.shape), -1, axis)


WIDE = False


def mx_kscale(k):
    if not WIDE:
        return np.ones(k)
    levels = np.array([10, -10, 5, -5, 0])
    if k % 512:
        return np.exp2(np.random.permutation(np.resize(levels, k // 32))).repeat(32)
    a = np.empty((k // 512, 16))
    for p in range(k // 512):
        a[p, :8] = np.random.permutation(np.resize(levels, 8))
        for g in range(8):
            far = levels[np.abs(levels - a[p, g]) >= 10]
            a[p, g + 8] = far[np.random.randint(len(far))]
    return np.exp2(a.ravel()).repeat(32)


def f64(x):
    return np.asarray(x).astype(np.float64)


def striped(idx):
    return np.tile(idx.reshape(-1, 16).T, (8, 1)).astype(np.uint16)


def unstriped(offs):
    return offs[:16].T.reshape(-1).astype(np.int64)


E2M1 = np.array([0.0, 0.5, 1.0, 1.5, 2.0, 3.0, 4.0, 6.0, -0.0, -0.5, -1.0, -1.5, -2.0, -3.0, -4.0, -6.0])


def pack_weight(w, fmt):
    k, n = w.shape
    w = f64(np.asarray(w, np.float32).astype(ml_dtypes.bfloat16)).reshape(k // 32, 32, n)
    amax = np.abs(w).max(1)
    if fmt == "e4m3":
        byte = np.frexp(amax)[1] - 1 + 127 - 7
    else:
        mant, ex = np.frexp(amax / 6.0)
        byte = np.where(mant > 0.5, ex, ex - 1) + 127
    byte = np.clip(np.where(amax > 0, byte, 1), 1, 254)
    scaled = (w * np.exp2(127.0 - byte)[:, None, :]).reshape(k, n).astype(np.float32)
    by_word = np.ascontiguousarray(scaled.reshape(k // 512, 128, 4, n).transpose(0, 1, 3, 2))
    if fmt == "e4m3":
        words = by_word.astype(ml_dtypes.float8_e4m3fn).view(np.uint8)
    else:
        c = by_word.astype(ml_dtypes.float4_e2m1fn).view(np.uint8) & 0xF
        words = (c[..., 0::2] | (c[..., 1::2] << 4)).reshape(k // 512, 128, 2 * n)
    return np.ascontiguousarray(words), np.ascontiguousarray(byte.astype(np.uint8).reshape(k // 512, 16, n))


def unpack_weight(words, scales, fmt):
    g, _, n = scales.shape
    words = np.ascontiguousarray(words).reshape(g, 128, n, -1)
    if fmt == "e4m3":
        vals = words.view(ml_dtypes.float8_e4m3fn).astype(np.float64)
    else:
        nib = np.empty((g, 128, n, 4), np.uint8)
        nib[..., 0::2] = words & 0xF
        nib[..., 1::2] = words >> 4
        vals = E2M1[nib]
    vals = vals * np.repeat(np.exp2(scales.astype(np.float64) - 127.0), 8, axis=1)[..., None]
    return vals.transpose(0, 1, 3, 2).reshape(g * 512, n)


def gelu(v):
    return 0.5 * v * (1.0 + np.tanh(np.sqrt(2.0 / np.pi) * (v + 0.044715 * v**3)))


K, K2, H, N, T, T3, S, P = 1536, 512, 1024, 384, 4096, 2048, 1024, 512

def setup_inputs():
    n = np.random.standard_normal
    s, s2, u = mx_kscale(K)[:, None], mx_kscale(K2)[:, None], mx_kscale(H)[:, None]
    d = {}
    d["tab_words"], d["tab_scales"] = pack_weight(n((K, T)) * s, "e4m3")
    d["tab2_words"], d["tab2_scales"] = pack_weight(n((K2, T3)) * s2, "e4m3")
    d["offs"] = striped(np.random.permutation(T)[:S])
    d["offs2"] = striped(np.random.permutation(T3)[:P])
    d["pos1"] = striped(np.random.permutation(S)[:P])
    d["w1"] = (n((K, H)) / s * u.T / K**0.5).astype(np.float32)
    d["w2_words"], d["w2_scales"] = pack_weight(n((K2, H)) / s2 / K2**0.5, "e2m1")
    d["gain"] = (np.exp(0.4 * n(H)) * u[:, 0]).astype(np.float32)
    d["wgs"] = np.exp(0.3 * n((128, P))).astype(np.float32)
    d["marks"] = (0.8 * n((H, S)) * u).astype(np.float32)
    d["w4_words"], d["w4_scales"] = pack_weight(0.8 * n((H, N)) / u / H**0.5, "e4m3")
    d["w5"] = (1.2 * n((H, N)) / u / H**0.5).astype(np.float32)
    return d

def reference(tab_words, tab_scales, tab2_words, tab2_scales, offs, offs2, pos1, w1, w2_words, w2_scales, gain, wgs, marks, w4_words, w4_scales, w5):
    v = unpack_weight(tab_words, tab_scales, "e4m3")[:, unstriped(offs)]
    v2 = unpack_weight(tab2_words, tab2_scales, "e4m3")[:, unstriped(offs2)]
    a = mxq(f64(w1), 0, "e4m3").T @ v
    b = f64(gain)[:, None] * (unpack_weight(w2_words, w2_scales, "e2m1").T @ v2)
    placed = np.zeros((H, S))
    placed[:, unstriped(pos1)] = np.tile(f64(wgs), (H // 128, 1)) * b
    z = np.abs(a - placed) + f64(marks)
    y = unpack_weight(w4_words, w4_scales, "e4m3").T @ mxq(z, 0, "e4m3")
    skip = mxq(f64(w5), 0, "e4m3").T @ mxq(a, 0, "e4m3")
    return np.minimum(y, skip)

@@ -1,0 +1,319 @@
+from contextlib import ExitStack
+
+import concourse.mybir as mybir
+
+K, K2, H, N, T, T3, S, PL = 1536, 512, 1024, 384, 4096, 2048, 1024, 512
+FLOPS = 2 * (K * H * S + K2 * H * PL + 2 * H * N * S)
+
+F32 = mybir.dt.float32
+BF16 = mybir.dt.bfloat16
+I32 = mybir.dt.int32
+U32 = mybir.dt.uint32
+U16 = mybir.dt.uint16
+U8 = mybir.dt.uint8
+FP8X4 = mybir.dt.float8_e4m3fn_x4
+FP4X4 = mybir.dt.float4_e2m1fn_x4
+ALU = mybir.AluOpType
+ACT = mybir.ActivationFunctionType
+
+P = 128
+PACK = 4
+KP = P * PACK
+PASSES = K // KP
+GROUPS = H // KP
+HALF = 512
+CHUNK = 256
+UNIT = 128
+SLICES = N // P
+
+
+def tile_list_parcel_conflict_scorer_kernel(
+    tc, tab_words, tab_scales, tab2_words, tab2_scales, offs, offs2, pos1, w1,
+    w2_words, w2_scales, gain, wgs, marks, w4_words, w4_scales, w5, out,
+):
+    nc = tc.nc
+    with ExitStack() as ctx:
+        keep = ctx.enter_context(tc.tile_pool(name="keep", bufs=1))
+        big = ctx.enter_context(tc.tile_pool(name="big", bufs=3))
+        ring = ctx.enter_context(tc.tile_pool(name="ring", bufs=3))
+        pair = ctx.enter_context(tc.tile_pool(name="pair", bufs=2))
+        psum = ctx.enter_context(tc.psum_pool(name="psum", bufs=4))
+
+        def kept(shape, dtype, name):
+            return keep.tile(shape, dtype, name=name, align_bytes=64)
+
+        offs_sb = keep.tile([P, S // 16], U16, name="offs_sb")
+        offs2_sb = keep.tile([P, PL // 16], U16, name="offs2_sb")
+        pos_sb = keep.tile([P, PL // 16], U16, name="pos_sb")
+
+        tab2_sc = kept([P, T3], U8, "tab2_sc")
+        tab_sc = kept([P, T], U8, "tab_sc")
+        w2_sc_raw = kept([P, H], U8, "w2_sc_raw")
+        w4_sc = kept([P, N], U8, "w4_sc")
+        nc.vector.memset(tab2_sc[:].bitcast(I32), 0)
+        nc.gpsimd.memset(w2_sc_raw[:].bitcast(I32), 0)
+        nc.gpsimd.memset(w4_sc[:].bitcast(I32), 0)
+        nc.vector.memset(tab_sc[:].bitcast(I32), 0)
+
+        def load_scales(queue, tile, src):
+            rows = PACK * src.shape[0]
+            for q in range(4):
+                queue.dma_start(
+                    out=tile[32 * q : 32 * q + rows, :].bitcast(I32),
+                    in_=src[:, 4 * q : 4 * q + 4, :].bitcast(I32),
+                )
+
+        tab2_w = ring.tile([P, T3], I32, name="tab2_w", tag="stream", align_bytes=64)
+        w2_raw = kept([P, 2 * H], U8, "w2_raw")
+        nc.sync.dma_start(offs2_sb[:], offs2)
+        nc.sync.dma_start(out=tab2_w[:], in_=tab2_words[0].rearrange("p t i -> p (t i)").bitcast(I32))
+        nc.sync.dma_start(out=w2_raw[:].bitcast(I32), in_=w2_words[0].bitcast(I32))
+        load_scales(nc.sync, tab2_sc, tab2_scales)
+        load_scales(nc.gpsimd, w2_sc_raw, w2_scales)
+        load_scales(nc.gpsimd, w4_sc, w4_scales)
+        nc.sync.dma_start(pos_sb[:], pos1)
+        gain_sb = kept([P, GROUPS, PACK], F32, "gain_sb")
+        nc.sync.dma_start(out=gain_sb[:], in_=gain.rearrange("(g p t) -> p g t", g=GROUPS, t=PACK))
+        wgs_sb = kept([P, PACK * PL], F32, "wgs_sb")
+        for q in range(4):
+            nc.sync.dma_start(
+                out=wgs_sb[32 * q : 32 * q + 32, :], in_=wgs.rearrange("(p t) m -> p (t m)", t=PACK)
+            )
+        nc.sync.dma_start(offs_sb[:], offs)
+        load_scales(nc.sync, tab_sc, tab_scales)
+
+        pages = [[kept([P, S], F32, f"page{g}{t}") for t in range(PACK)] for g in range(GROUPS)]
+        for t in range(PACK):
+            nc.vector.memset(pages[0][t][:], 0.0)
+        for t in range(PACK):
+            nc.gpsimd.memset(pages[1][t][:], 0.0)
+
+        tab_w = []
+        for a in range(PASSES):
+            tile = big.tile([P, T], I32, name=f"tab_w{a}", tag="big", align_bytes=64)
+            nc.sync.dma_start(out=tile[:], in_=tab_words[a].rearrange("p t i -> p (t i)").bitcast(I32))
+            tab_w.append(tile)
+
+        w2_c = kept([P, 2 * H], U8, "w2_c")
+        w2_sc = kept([P, H], U8, "w2_sc")
+        nc.vector.tensor_copy(
+            out=w2_c[:].rearrange("p (g t m b) -> p g m t b", g=GROUPS, t=PACK, b=2),
+            in_=w2_raw[:].rearrange("p (g m t b) -> p g m t b", g=GROUPS, t=PACK, b=2),
+        )
+        nc.vector.tensor_copy(
+            out=w2_sc[:].rearrange("p (g t m) -> p g m t", g=GROUPS, t=PACK),
+            in_=w2_sc_raw[:].rearrange("p (g m t) -> p g m t", g=GROUPS, t=PACK),
+        )
+        v2 = kept([P, PL], U32, "v2")
+        v2_sc = kept([P, PL], U8, "v2_sc")
+        nc.vector.tensor_copy(v2[:], tab2_w[:].bitcast(U32).indirect(offs2_sb[:]))
+        nc.vector.tensor_copy(v2_sc[:], tab2_sc[:].indirect(offs2_sb[:]))
+
+        def place(g, t):
+            s = PACK * g + t
+            bank = psum.tile([P, PL], F32, name="b_ps", tag="late")
+            nc.tensor.matmul_mx(
+                out=bank[:],
+                lhsT=w2_c[:, 2 * P * s : 2 * P * (s + 1)].bitcast(FP4X4),
+                lhsT_scale=w2_sc[:, P * s : P * (s + 1)],
+                rhs=v2[:].bitcast(FP8X4),
+                rhs_scale=v2_sc[:],
+                start=True,
+                stop=True,
+            )
+            b_sb = pair.tile([P, PL], F32, name="b_sb")
+            nc.scalar.activation(out=b_sb[:], in_=bank[:], func=ACT.Copy, scale=gain_sb[:, g, t : t + 1])
+            nc.vector.tensor_tensor(
+                pages[g][t][:].indirect(pos_sb[:]), b_sb[:], wgs_sb[:, PL * t : PL * (t + 1)], ALU.mult
+            )
+
+        for t in range(PACK):
+            place(0, t)
+
+        v = [[kept([P, HALF], U32, f"v{h}{a}") for a in range(PASSES)] for h in range(S // HALF)]
+        v_sc = [kept([P, HALF], U8, f"v_sc{h}") for h in range(S // HALF)]
+
+        def gather(h):
+            cols = offs_sb[:, h * HALF // 16 : (h + 1) * HALF // 16]
+            nc.vector.tensor_copy(v_sc[h][:], tab_sc[:].indirect(cols))
+            for a in range(PASSES):
+                nc.vector.tensor_copy(v[h][a][:], tab_w[a][:].bitcast(U32).indirect(cols))
+
+        w1_c = [[kept([P, KP], U32, f"w1_c{g}{a}") for a in range(PASSES)] for g in range(GROUPS)]
+        w1_sc = [[kept([P, KP], U8, f"w1_sc{g}{a}") for a in range(PASSES)] for g in range(GROUPS)]
+
+        def quantise_w1(g, a):
+            raw = ring.tile([P, PACK, KP], F32, name="w1_raw", tag="stream", align_bytes=64)
+            nc.sync.dma_start(
+                out=raw[:],
+                in_=w1[KP * a : KP * (a + 1), KP * g : KP * (g + 1)].rearrange("(p i) c -> p i c", i=PACK),
+            )
+            w16 = pair.tile([P, KP * PACK], BF16, name="w1_16", tag="w16", align_bytes=64)
+            nc.scalar.copy(
+                out=w16[:].rearrange("p (t m i) -> p m i t", t=PACK, i=PACK),
+                in_=raw[:].rearrange("p i (m t) -> p m i t", t=PACK),
+            )
+            nc.vector.quantize_mx(out=w1_c[g][a][:].bitcast(FP8X4), scales=w1_sc[g][a][:], in_=w16[:])
+
+        w5_c = [kept([P, N], U32, f"w5_c{g}") for g in range(GROUPS)]
+        w5_sc = [kept([P, N], U8, f"w5_sc{g}") for g in range(GROUPS)]
+
+        def quantise_w5(g):
+            raw = ring.tile([P, PACK, N], F32, name="w5_raw", tag="stream", align_bytes=64)
+            nc.sync.dma_start(
+                out=raw[:], in_=w5[KP * g : KP * (g + 1), :].rearrange("(p i) c -> p i c", i=PACK)
+            )
+            w16 = pair.tile([P, N * PACK], BF16, name="w5_16", tag="w16", align_bytes=64)
+            nc.scalar.copy(
+                out=w16[:].rearrange("p (c e i) -> p c i e", e=2, i=PACK),
+                in_=raw[:].rearrange("p i (c e) -> p c i e", e=2),
+            )
+            for c0, c1 in ((0, 256), (256, N)):
+                nc.vector.quantize_mx(
+                    out=w5_c[g][:, c0:c1].bitcast(FP8X4),
+                    scales=w5_sc[g][:, c0:c1],
+                    in_=w16[:, PACK * c0 : PACK * c1],
+                )
+
+        marks_sb = {}
+
+        def load_marks(g, h):
+            tile = ring.tile([P, PACK, HALF], F32, name="marks_sb", tag="marks")
+            nc.sync.dma_start(
+                out=tile[:],
+                in_=marks[KP * g : KP * (g + 1), HALF * h : HALF * (h + 1)].rearrange("(p t) j -> p t j", t=PACK),
+            )
+            marks_sb[g, h] = tile
+
+        gather(0)
+        for a in range(PASSES):
+            quantise_w1(0, a)
+        gather(1)
+        load_marks(0, 0)
+        load_marks(0, 1)
+        for t in range(PACK):
+            place(1, t)
+        for a in range(PASSES):
+            quantise_w1(1, a)
+        w4_c = kept([P, GROUPS, N], I32, "w4_c")
+        nc.sync.dma_start(out=w4_c[:], in_=w4_words.rearrange("a p c i -> p a (c i)").bitcast(I32))
+        for g in range(GROUPS):
+            quantise_w5(g)
+        load_marks(1, 0)
+        load_marks(1, 1)
+
+        codes = big.tile([P, 2 * GROUPS * S], U32, name="codes", tag="big", align_bytes=64)
+        scales = kept([P, 2 * GROUPS * S], U8, "scales")
+        result = big.tile([P, SLICES * S], F32, name="result", tag="big", align_bytes=64)
+
+        def cols_of(which, g, c):
+            start = (2 * g + which) * S + c * CHUNK
+            return slice(start, start + CHUNK)
+
+        units = [(g, u) for g in range(GROUPS) for u in range(S // UNIT)]
+        per_chunk = CHUNK // UNIT
+        a16, z16, diff = {}, {}, {}
+
+        def paired(ap3):
+            return ap3.rearrange("p t (c e) -> p c t e", e=2)
+
+        def woven(tile, u):
+            first = (u % per_chunk) * UNIT * PACK
+            return tile[:, first : first + UNIT * PACK].rearrange("p (c e t) -> p c t e", e=2, t=PACK)
+
+        def quantise(which, g, c, tile):
+            nc.vector.quantize_mx(
+                out=codes[:, cols_of(which, g, c)].bitcast(FP8X4),
+                scales=scales[:, cols_of(which, g, c)],
+                in_=tile[:],
+            )
+
+        def front(g, u):
+            h, j0 = divmod(u * UNIT, HALF)
+            bank = psum.tile([P, PACK, UNIT], F32, name="a_ps", tag="a")
+            for t in range(PACK):
+                for a in range(PASSES):
+                    nc.tensor.matmul_mx(
+                        out=bank[:, t, :],
+                        lhsT=w1_c[g][a][:, P * t : P * (t + 1)].bitcast(FP8X4),
+                        lhsT_scale=w1_sc[g][a][:, P * t : P * (t + 1)],
+                        rhs=v[h][a][:, j0 : j0 + UNIT].bitcast(FP8X4),
+                        rhs_scale=v_sc[h][PACK * a : P, j0 : j0 + UNIT],
+                        start=(a == 0),
+                        stop=(a == PASSES - 1),
+                    )
+            d = ring.tile([P, PACK, UNIT], F32, name="diff")
+            for t in range(PACK):
+                nc.vector.tensor_tensor(
+                    d[:, t, :], bank[:, t, :], pages[g][t][:, u * UNIT : (u + 1) * UNIT], ALU.subtract
+                )
+            diff[g, u] = d
+            c = u // per_chunk
+            if u % per_chunk == 0:
+                a16[g, c] = pair.tile([P, CHUNK * PACK], BF16, name="a16", align_bytes=64)
+            nc.scalar.activation(out=d[:], in_=d[:], func=ACT.Abs)
+            nc.scalar.copy(out=woven(a16[g, c], u), in_=paired(bank[:]))
+
+        def back(g, u):
+            h, j0 = divmod(u * UNIT, HALF)
+            c = u // per_chunk
+            if u % per_chunk == 0:
+                z16[g, c] = pair.tile([P, CHUNK * PACK], BF16, name="z16", align_bytes=64)
+            nc.vector.tensor_tensor(
+                woven(z16[g, c], u),
+                paired(diff[g, u][:]),
+                paired(marks_sb[g, h][:, :, j0 : j0 + UNIT]),
+                ALU.add,
+            )
+
+        def scores(which, weights, weight_scales, c, s):
+            bank = psum.tile([P, CHUNK], F32, name="score_ps", tag="late")
+            for g in range(GROUPS):
+                nc.tensor.matmul_mx(
+                    out=bank[:],
+                    lhsT=weights(g)[:, P * s : P * (s + 1)].bitcast(FP8X4),
+                    lhsT_scale=weight_scales(g)[:, P * s : P * (s + 1)],
+                    rhs=codes[:, cols_of(which, g, c)].bitcast(FP8X4),
+                    rhs_scale=scales[:, cols_of(which, g, c)],
+                    start=(g == 0),
+                    stop=(g == GROUPS - 1),
+                )
+            return bank
+
+        skip_sb = {}
+
+        def finish_skip(c):
+            tile = pair.tile([P, SLICES, CHUNK], F32, name="skip_sb")
+            for s in range(SLICES):
+                bank = scores(0, lambda g: w5_c[g][:], lambda g: w5_sc[g][:], c, s)
+                nc.scalar.copy(out=tile[:, s, :], in_=bank[:])
+            skip_sb[c] = tile
+
+        def finish(c):
+            res = result[:, c * SLICES * CHUNK : (c + 1) * SLICES * CHUNK].rearrange("p (s j) -> p s j", s=SLICES)
+            for s in range(SLICES):
+                bank = scores(1, lambda g: w4_c[:, g, :], lambda g: w4_sc[PACK * g : P, :], c, s)
+                nc.vector.tensor_tensor(res[:, s, :], bank[:], skip_sb[c][:, s, :], ALU.min)
+            nc.sync.dma_start(
+                out=out[:, c * CHUNK : (c + 1) * CHUNK].rearrange("(s p) j -> p s j", p=P), in_=res
+            )
+
+        last = per_chunk - 1
+        for step in range(len(units) + 3):
+            if step < len(units):
+                front(*units[step])
+            if 1 <= step <= len(units):
+                g, u = units[step - 1]
+                back(g, u)
+                if u % per_chunk == last:
+                    quantise(0, g, u // per_chunk, a16[g, u // per_chunk])
+            if 2 <= step <= len(units) + 1:
+                g, u = units[step - 2]
+                if u % per_chunk == last:
+                    quantise(1, g, u // per_chunk, z16[g, u // per_chunk])
+                    if g == GROUPS - 1:
+                        finish_skip(u // per_chunk)
+            if step >= 3:
+                g, u = units[step - 3]
+                if u % per_chunk == last and g == GROUPS - 1:
+                    finish(u // per_chunk)

@@ -1,6 +1,7 @@
 from contextlib import ExitStack
 
 import concourse.mybir as mybir
+from concourse.masks import make_identity
 
 K, K2, H, N, T, T3, S, PL = 1536, 512, 1024, 384, 4096, 2048, 1024, 512
 FLOPS = 2 * (K * H * S + K2 * H * PL + 2 * H * N * S)
@@ -25,6 +26,12 @@ HALF = 512
 CHUNK = 256
 UNIT = 128
 SLICES = N // P
+YTAG = "turn_ps"
+HELD = [1,2]
+W1S = [2, 4, 6]
+W5S = [3,6]
+STG = [-1,-1,0,2]
+TRN = [0,1,2,3,4,5,6,7]
 
 
 def tile_list_parcel_conflict_scorer_kernel(
@@ -35,9 +42,10 @@ def tile_list_parcel_conflict_scorer_kernel(
     with ExitStack() as ctx:
         keep = ctx.enter_context(tc.tile_pool(name="keep", bufs=1))
         big = ctx.enter_context(tc.tile_pool(name="big", bufs=3))
-        ring = ctx.enter_context(tc.tile_pool(name="ring", bufs=3))
+        quad = ctx.enter_context(tc.tile_pool(name="quad", bufs=4))
+        six = ctx.enter_context(tc.tile_pool(name="six", bufs=6))
         pair = ctx.enter_context(tc.tile_pool(name="pair", bufs=2))
-        psum = ctx.enter_context(tc.psum_pool(name="psum", bufs=4))
+        psum = ctx.enter_context(tc.psum_pool(name="psum", bufs=2))
 
         def kept(shape, dtype, name):
             return keep.tile(shape, dtype, name=name, align_bytes=64)
@@ -51,9 +59,11 @@ def tile_list_parcel_conflict_scorer_kernel(
         w2_sc_raw = kept([P, H], U8, "w2_sc_raw")
         w4_sc = kept([P, N], U8, "w4_sc")
         nc.vector.memset(tab2_sc[:].bitcast(I32), 0)
-        nc.gpsimd.memset(w2_sc_raw[:].bitcast(I32), 0)
-        nc.gpsimd.memset(w4_sc[:].bitcast(I32), 0)
+        nc.vector.memset(w2_sc_raw[:].bitcast(I32), 0)
         nc.vector.memset(tab_sc[:].bitcast(I32), 0)
+        nc.vector.memset(w4_sc[:].bitcast(I32), 0)
+        ident = kept([P, P], F32, "ident")
+        make_identity(nc, ident[:])
 
         def load_scales(queue, tile, src):
             rows = PACK * src.shape[0]
@@ -63,54 +73,45 @@ def tile_list_parcel_conflict_scorer_kernel(
                     in_=src[:, 4 * q : 4 * q + 4, :].bitcast(I32),
                 )
 
-        tab2_w = ring.tile([P, T3], I32, name="tab2_w", tag="stream", align_bytes=64)
+        tab2_w = six.tile([P, T3], I32, name="tab2_w", tag="stream", align_bytes=64)
         w2_raw = kept([P, 2 * H], U8, "w2_raw")
-        nc.sync.dma_start(offs2_sb[:], offs2)
-        nc.sync.dma_start(out=tab2_w[:], in_=tab2_words[0].rearrange("p t i -> p (t i)").bitcast(I32))
-        nc.sync.dma_start(out=w2_raw[:].bitcast(I32), in_=w2_words[0].bitcast(I32))
-        load_scales(nc.sync, tab2_sc, tab2_scales)
-        load_scales(nc.gpsimd, w2_sc_raw, w2_scales)
-        load_scales(nc.gpsimd, w4_sc, w4_scales)
-        nc.sync.dma_start(pos_sb[:], pos1)
         gain_sb = kept([P, GROUPS, PACK], F32, "gain_sb")
+        nc.sync.dma_start(offs2_sb[:], offs2)
+        nc.sync.dma_start(pos_sb[:], pos1)
         nc.sync.dma_start(out=gain_sb[:], in_=gain.rearrange("(g p t) -> p g t", g=GROUPS, t=PACK))
+        nc.sync.dma_start(offs_sb[:], offs)
+        nc.sync.dma_start(out=w2_raw[:].bitcast(I32), in_=w2_words[0].bitcast(I32))
+        nc.sync.dma_start(out=tab2_w[:], in_=tab2_words[0].rearrange("p t i -> p (t i)").bitcast(I32))
+        load_scales(nc.sync, tab2_sc, tab2_scales)
+        load_scales(nc.sync, w2_sc_raw, w2_scales)
         wgs_sb = kept([P, PACK * PL], F32, "wgs_sb")
         for q in range(4):
             nc.sync.dma_start(
                 out=wgs_sb[32 * q : 32 * q + 32, :], in_=wgs.rearrange("(p t) m -> p (t m)", t=PACK)
             )
-        nc.sync.dma_start(offs_sb[:], offs)
-        load_scales(nc.sync, tab_sc, tab_scales)
-
         pages = [[kept([P, S], F32, f"page{g}{t}") for t in range(PACK)] for g in range(GROUPS)]
-        for t in range(PACK):
-            nc.vector.memset(pages[0][t][:], 0.0)
-        for t in range(PACK):
-            nc.gpsimd.memset(pages[1][t][:], 0.0)
-
-        tab_w = []
-        for a in range(PASSES):
-            tile = big.tile([P, T], I32, name=f"tab_w{a}", tag="big", align_bytes=64)
-            nc.sync.dma_start(out=tile[:], in_=tab_words[a].rearrange("p t i -> p (t i)").bitcast(I32))
-            tab_w.append(tile)
 
         w2_c = kept([P, 2 * H], U8, "w2_c")
         w2_sc = kept([P, H], U8, "w2_sc")
-        nc.vector.tensor_copy(
-            out=w2_c[:].rearrange("p (g t m b) -> p g m t b", g=GROUPS, t=PACK, b=2),
-            in_=w2_raw[:].rearrange("p (g m t b) -> p g m t b", g=GROUPS, t=PACK, b=2),
-        )
-        nc.vector.tensor_copy(
-            out=w2_sc[:].rearrange("p (g t m) -> p g m t", g=GROUPS, t=PACK),
-            in_=w2_sc_raw[:].rearrange("p (g m t) -> p g m t", g=GROUPS, t=PACK),
-        )
         v2 = kept([P, PL], U32, "v2")
         v2_sc = kept([P, PL], U8, "v2_sc")
         nc.vector.tensor_copy(v2[:], tab2_w[:].bitcast(U32).indirect(offs2_sb[:]))
         nc.vector.tensor_copy(v2_sc[:], tab2_sc[:].indirect(offs2_sb[:]))
 
-        def place(g, t):
+        def deal_w2(g):
+            words, cols = slice(2 * KP * g, 2 * KP * (g + 1)), slice(KP * g, KP * (g + 1))
+            nc.vector.tensor_copy(
+                out=w2_c[:, words].rearrange("p (t m b) -> p m t b", t=PACK, b=2),
+                in_=w2_raw[:, words].rearrange("p (m t b) -> p m t b", t=PACK, b=2),
+            )
+            nc.vector.tensor_copy(
+                out=w2_sc[:, cols].rearrange("p (t m) -> p m t", t=PACK),
+                in_=w2_sc_raw[:, cols].rearrange("p (m t) -> p m t", t=PACK),
+            )
+
+        def place(g, t, b_sb):
             s = PACK * g + t
+            nc.vector.memset(pages[g][t][:], 0.0)
             bank = psum.tile([P, PL], F32, name="b_ps", tag="late")
             nc.tensor.matmul_mx(
                 out=bank[:],
@@ -121,34 +122,34 @@ def tile_list_parcel_conflict_scorer_kernel(
                 start=True,
                 stop=True,
             )
-            b_sb = pair.tile([P, PL], F32, name="b_sb")
-            nc.scalar.activation(out=b_sb[:], in_=bank[:], func=ACT.Copy, scale=gain_sb[:, g, t : t + 1])
+            nc.scalar.activation(out=b_sb, in_=bank[:], func=ACT.Copy, scale=gain_sb[:, g, t : t + 1])
             nc.vector.tensor_tensor(
-                pages[g][t][:].indirect(pos_sb[:]), b_sb[:], wgs_sb[:, PL * t : PL * (t + 1)], ALU.mult
+                pages[g][t][:].indirect(pos_sb[:]), b_sb, wgs_sb[:, PL * t : PL * (t + 1)], ALU.mult
             )
 
-        for t in range(PACK):
-            place(0, t)
-
-        v = [[kept([P, HALF], U32, f"v{h}{a}") for a in range(PASSES)] for h in range(S // HALF)]
+        v = {}
         v_sc = [kept([P, HALF], U8, f"v_sc{h}") for h in range(S // HALF)]
 
-        def gather(h):
-            cols = offs_sb[:, h * HALF // 16 : (h + 1) * HALF // 16]
-            nc.vector.tensor_copy(v_sc[h][:], tab_sc[:].indirect(cols))
-            for a in range(PASSES):
-                nc.vector.tensor_copy(v[h][a][:], tab_w[a][:].bitcast(U32).indirect(cols))
+        def entries(h):
+            return offs_sb[:, h * HALF // 16 : (h + 1) * HALF // 16]
+
+        def gather(h, a):
+            v[h, a] = keep.tile([P, HALF], U32, name="v", tag=f"v{h}{a}", align_bytes=64)
+            nc.vector.tensor_copy(v[h, a][:], tab_w[a][:].bitcast(U32).indirect(entries(h)))
 
         w1_c = [[kept([P, KP], U32, f"w1_c{g}{a}") for a in range(PASSES)] for g in range(GROUPS)]
         w1_sc = [[kept([P, KP], U8, f"w1_sc{g}{a}") for a in range(PASSES)] for g in range(GROUPS)]
 
-        def quantise_w1(g, a):
-            raw = ring.tile([P, PACK, KP], F32, name="w1_raw", tag="stream", align_bytes=64)
+        def load_w1(g, a):
+            raw = six.tile([P, PACK, KP], F32, name="w1_raw", tag="stream", align_bytes=64)
             nc.sync.dma_start(
                 out=raw[:],
                 in_=w1[KP * a : KP * (a + 1), KP * g : KP * (g + 1)].rearrange("(p i) c -> p i c", i=PACK),
             )
-            w16 = pair.tile([P, KP * PACK], BF16, name="w1_16", tag="w16", align_bytes=64)
+            return raw
+
+        def quantise_w1(g, a, raw):
+            w16 = six.tile([P, KP * PACK], BF16, name="w1_16", tag="w16", align_bytes=64)
             nc.scalar.copy(
                 out=w16[:].rearrange("p (t m i) -> p m i t", t=PACK, i=PACK),
                 in_=raw[:].rearrange("p i (m t) -> p m i t", t=PACK),
@@ -158,12 +159,15 @@ def tile_list_parcel_conflict_scorer_kernel(
         w5_c = [kept([P, N], U32, f"w5_c{g}") for g in range(GROUPS)]
         w5_sc = [kept([P, N], U8, f"w5_sc{g}") for g in range(GROUPS)]
 
-        def quantise_w5(g):
-            raw = ring.tile([P, PACK, N], F32, name="w5_raw", tag="stream", align_bytes=64)
+        def load_w5(g):
+            raw = six.tile([P, PACK, N], F32, name="w5_raw", tag="stream", align_bytes=64)
             nc.sync.dma_start(
                 out=raw[:], in_=w5[KP * g : KP * (g + 1), :].rearrange("(p i) c -> p i c", i=PACK)
             )
-            w16 = pair.tile([P, N * PACK], BF16, name="w5_16", tag="w16", align_bytes=64)
+            return raw
+
+        def quantise_w5(g, raw):
+            w16 = six.tile([P, N * PACK], BF16, name="w5_16", tag="w16", align_bytes=64)
             nc.scalar.copy(
                 out=w16[:].rearrange("p (c e i) -> p c i e", e=2, i=PACK),
                 in_=raw[:].rearrange("p i (c e) -> p c i e", e=2),
@@ -178,27 +182,43 @@ def tile_list_parcel_conflict_scorer_kernel(
         marks_sb = {}
 
         def load_marks(g, h):
-            tile = ring.tile([P, PACK, HALF], F32, name="marks_sb", tag="marks")
+            tile = six.tile([P, PACK, HALF], F32, name="marks_sb", tag="stream", align_bytes=64)
             nc.sync.dma_start(
                 out=tile[:],
                 in_=marks[KP * g : KP * (g + 1), HALF * h : HALF * (h + 1)].rearrange("(p t) j -> p t j", t=PACK),
             )
             marks_sb[g, h] = tile
 
-        gather(0)
-        for a in range(PASSES):
-            quantise_w1(0, a)
-        gather(1)
-        load_marks(0, 0)
-        load_marks(0, 1)
+        deal_w2(0)
         for t in range(PACK):
-            place(1, t)
+            b_first = quad.tile([P, PL], F32, name="b_first", tag="a32")
+            place(0, t, b_first[:])
+        deal_w2(1)
+        for t in range(PACK):
+            if STG[t] < 0:
+                b_first = quad.tile([P, PL], F32, name="b_first", tag="diff")
+                place(1, t, b_first[:])
+        for g in range(GROUPS):
+            for a in range(PASSES):
+                quantise_w1(g, a, load_w1(g, a))
+        load_scales(nc.sync, tab_sc, tab_scales)
+        tab_w = []
         for a in range(PASSES):
-            quantise_w1(1, a)
+            tile = big.tile([P, T], I32, name=f"tab_w{a}", tag="big", align_bytes=64)
+            nc.sync.dma_start(out=tile[:], in_=tab_words[a].rearrange("p t i -> p (t i)").bitcast(I32))
+            tab_w.append(tile)
+        for h in range(S // HALF):
+            nc.vector.tensor_copy(v_sc[h][:], tab_sc[:].indirect(entries(h)))
+        for a in range(PASSES):
+            gather(0, a)
+            if a not in HELD:
+                gather(1, a)
+        load_marks(0, 0)
+        w5_later = [load_w5(g) for g in range(GROUPS)]
+        load_marks(0, 1)
+        load_scales(nc.sync, w4_sc, w4_scales)
         w4_c = kept([P, GROUPS, N], I32, "w4_c")
         nc.sync.dma_start(out=w4_c[:], in_=w4_words.rearrange("a p c i -> p a (c i)").bitcast(I32))
-        for g in range(GROUPS):
-            quantise_w5(g)
         load_marks(1, 0)
         load_marks(1, 1)
 
@@ -207,28 +227,35 @@ def tile_list_parcel_conflict_scorer_kernel(
         result = big.tile([P, SLICES * S], F32, name="result", tag="big", align_bytes=64)
 
         def cols_of(which, g, c):
-            start = (2 * g + which) * S + c * CHUNK
+            start = 2 * (g * S + c * CHUNK) + which * CHUNK
             return slice(start, start + CHUNK)
 
         units = [(g, u) for g in range(GROUPS) for u in range(S // UNIT)]
         per_chunk = CHUNK // UNIT
-        a16, z16, diff = {}, {}, {}
+        az16, diff, a32 = {}, {}, {}
+
+        staged = STG
+
+        def turned(k):
+            return k in TRN
 
         def paired(ap3):
             return ap3.rearrange("p t (c e) -> p c t e", e=2)
 
-        def woven(tile, u):
-            first = (u % per_chunk) * UNIT * PACK
-            return tile[:, first : first + UNIT * PACK].rearrange("p (c e t) -> p c t e", e=2, t=PACK)
+        def part(which, g, u):
+            first = (which * CHUNK + (u % per_chunk) * UNIT) * PACK
+            return az16[g, u // per_chunk][:, first : first + UNIT * PACK]
 
-        def quantise(which, g, c, tile):
+        def quantise(first, count, g, c):
+            cols = slice(cols_of(first, g, c).start, cols_of(first + count - 1, g, c).stop)
             nc.vector.quantize_mx(
-                out=codes[:, cols_of(which, g, c)].bitcast(FP8X4),
-                scales=scales[:, cols_of(which, g, c)],
-                in_=tile[:],
+                out=codes[:, cols].bitcast(FP8X4),
+                scales=scales[:, cols],
+                in_=az16[g, c][:, first * CHUNK * PACK : (first + count) * CHUNK * PACK],
             )
 
-        def front(g, u):
+        def product(k):
+            g, u = units[k]
             h, j0 = divmod(u * UNIT, HALF)
             bank = psum.tile([P, PACK, UNIT], F32, name="a_ps", tag="a")
             for t in range(PACK):
@@ -237,37 +264,65 @@ def tile_list_parcel_conflict_scorer_kernel(
                         out=bank[:, t, :],
                         lhsT=w1_c[g][a][:, P * t : P * (t + 1)].bitcast(FP8X4),
                         lhsT_scale=w1_sc[g][a][:, P * t : P * (t + 1)],
-                        rhs=v[h][a][:, j0 : j0 + UNIT].bitcast(FP8X4),
+                        rhs=v[h, a][:, j0 : j0 + UNIT].bitcast(FP8X4),
                         rhs_scale=v_sc[h][PACK * a : P, j0 : j0 + UNIT],
                         start=(a == 0),
                         stop=(a == PASSES - 1),
                     )
-            d = ring.tile([P, PACK, UNIT], F32, name="diff")
-            for t in range(PACK):
-                nc.vector.tensor_tensor(
-                    d[:, t, :], bank[:, t, :], pages[g][t][:, u * UNIT : (u + 1) * UNIT], ALU.subtract
-                )
-            diff[g, u] = d
-            c = u // per_chunk
             if u % per_chunk == 0:
-                a16[g, c] = pair.tile([P, CHUNK * PACK], BF16, name="a16", align_bytes=64)
-            nc.scalar.activation(out=d[:], in_=d[:], func=ACT.Abs)
-            nc.scalar.copy(out=woven(a16[g, c], u), in_=paired(bank[:]))
+                az16[g, u // per_chunk] = six.tile([P, 2 * CHUNK * PACK], BF16, name="az16", tag="w16", align_bytes=64)
+            if turned(k):
+                if k < len(HELD):
+                    a32[k] = keep.tile([P, PACK, UNIT], F32, name="a32", tag=f"v1{HELD[k]}", align_bytes=64)
+                else:
+                    a32[k] = quad.tile([P, PACK, UNIT], F32, name="a32", tag="a32")
+                nc.scalar.activation(out=a32[k][:], in_=bank[:], func=ACT.Copy, scale=-1.0)
+            else:
+                diff[k] = quad.tile([P, PACK, UNIT], F32, name="diff")
+                for t in range(PACK):
+                    nc.vector.tensor_tensor(
+                        diff[k][:, t, :], bank[:, t, :], pages[g][t][:, u * UNIT : (u + 1) * UNIT], ALU.subtract
+                    )
+                nc.scalar.activation(out=diff[k][:], in_=diff[k][:], func=ACT.Abs)
+            nc.scalar.copy(
+                out=part(0, g, u).rearrange("p (n t) -> p n t", t=PACK), in_=bank[:].rearrange("p t n -> p n t")
+            )
 
-        def back(g, u):
+        def turn(k):
+            g, u = units[k]
+            bank = psum.tile([P, PACK, P], F32, name="turn_ps")
+            for t in range(PACK):
+                nc.tensor.matmul(
+                    out=bank[:, t, :], lhsT=pages[g][t][:, u * UNIT : (u + 1) * UNIT], rhs=ident[:],
+                    is_transpose=True, start=True, stop=False,
+                )
+                nc.tensor.matmul(
+                    out=bank[:, t, :], lhsT=a32[k][:, t, :], rhs=ident[:],
+                    is_transpose=True, start=False, stop=True,
+                )
+            diff[k] = quad.tile([P, PACK, UNIT], F32, name="diff")
+            nc.scalar.activation(out=diff[k][:], in_=bank[:], func=ACT.Abs)
+
+        def turn_back(k):
+            bank = psum.tile([P, PACK, UNIT], F32, name="back_ps")
+            for t in range(PACK):
+                nc.tensor.transpose(bank[:, t, :], diff[k][:, t, :], ident[:])
+            if k in staged:
+                place(1, staged.index(k), diff[k][:].rearrange("p t n -> p (t n)"))
+            diff[k] = bank
+
+        def add_marks(k):
+            g, u = units[k]
             h, j0 = divmod(u * UNIT, HALF)
-            c = u // per_chunk
-            if u % per_chunk == 0:
-                z16[g, c] = pair.tile([P, CHUNK * PACK], BF16, name="z16", align_bytes=64)
             nc.vector.tensor_tensor(
-                woven(z16[g, c], u),
-                paired(diff[g, u][:]),
+                part(1, g, u).rearrange("p (c e t) -> p c t e", e=2, t=PACK),
+                paired(diff[k][:]),
                 paired(marks_sb[g, h][:, :, j0 : j0 + UNIT]),
                 ALU.add,
             )
 
         def scores(which, weights, weight_scales, c, s):
-            bank = psum.tile([P, CHUNK], F32, name="score_ps", tag="late")
+            bank = psum.tile([P, CHUNK], F32, name="score_ps", tag="late" if which == 0 else YTAG)
             for g in range(GROUPS):
                 nc.tensor.matmul_mx(
                     out=bank[:],
@@ -298,22 +353,29 @@ def tile_list_parcel_conflict_scorer_kernel(
                 out=out[:, c * CHUNK : (c + 1) * CHUNK].rearrange("(s p) j -> p s j", p=P), in_=res
             )
 
-        last = per_chunk - 1
-        for step in range(len(units) + 3):
+        def chunk_end(k):
+            return 0 <= k < len(units) and units[k][1] % per_chunk == per_chunk - 1
+
+        for step in range(len(units) + 5):
             if step < len(units):
-                front(*units[step])
-            if 1 <= step <= len(units):
-                g, u = units[step - 1]
-                back(g, u)
-                if u % per_chunk == last:
-                    quantise(0, g, u // per_chunk, a16[g, u // per_chunk])
-            if 2 <= step <= len(units) + 1:
-                g, u = units[step - 2]
-                if u % per_chunk == last:
-                    quantise(1, g, u // per_chunk, z16[g, u // per_chunk])
-                    if g == GROUPS - 1:
-                        finish_skip(u // per_chunk)
-            if step >= 3:
+                product(step)
+            if turned(step - 1):
+                turn(step - 1)
+            if 0 <= step - 1 < len(HELD):
+                gather(1, HELD[step - 1])
+            if turned(step - 2):
+                turn_back(step - 2)
+            if chunk_end(step - 1) and units[step - 1][0] == GROUPS - 1:
+                quantise(0, 1, GROUPS - 1, units[step - 1][1] // per_chunk)
+                finish_skip(units[step - 1][1] // per_chunk)
+            if 0 <= step - 2 < len(units):
+                add_marks(step - 2)
+            if step in W5S:
+                quantise_w5(W5S.index(step), w5_later[W5S.index(step)])
+            if chunk_end(step - 3):
                 g, u = units[step - 3]
-                if u % per_chunk == last and g == GROUPS - 1:
+                if g == GROUPS - 1:
+                    quantise(1, 1, g, u // per_chunk)
                     finish(u // per_chunk)
+                else:
+                    quantise(0, 2, g, u // per_chunk)

@@ -27,10 +27,10 @@ CHUNK = 256
 UNIT = 128
 SLICES = N // P
 YTAG = "turn_ps"
-HELD = [1,2]
-W1S = [2, 4, 6]
-W5S = [3,6]
-STG = [-1,-1,0,2]
+HELD = [0,1]
+SPLIT = -1
+W5S = [4,7]
+STG = [-1,-2,0,2]
 TRN = [0,1,2,3,4,5,6,7]
 
 
@@ -101,17 +101,17 @@ def tile_list_parcel_conflict_scorer_kernel(
         def deal_w2(g):
             words, cols = slice(2 * KP * g, 2 * KP * (g + 1)), slice(KP * g, KP * (g + 1))
             nc.vector.tensor_copy(
-                out=w2_c[:, words].rearrange("p (t m b) -> p m t b", t=PACK, b=2),
-                in_=w2_raw[:, words].rearrange("p (m t b) -> p m t b", t=PACK, b=2),
+                out=w2_c[:, words].rearrange("p (t m b) -> p t m b", t=PACK, b=2),
+                in_=w2_raw[:, words].rearrange("p (m t b) -> p t m b", t=PACK, b=2),
             )
             nc.vector.tensor_copy(
-                out=w2_sc[:, cols].rearrange("p (t m) -> p m t", t=PACK),
-                in_=w2_sc_raw[:, cols].rearrange("p (m t) -> p m t", t=PACK),
+                out=w2_sc[:, cols].rearrange("p (t m) -> p t m", t=PACK),
+                in_=w2_sc_raw[:, cols].rearrange("p (m t) -> p t m", t=PACK),
             )
 
         def place(g, t, b_sb):
             s = PACK * g + t
-            nc.vector.memset(pages[g][t][:], 0.0)
+            nc.vector.memset(pages[g][t][:].bitcast(I32), 0)
             bank = psum.tile([P, PL], F32, name="b_ps", tag="late")
             nc.tensor.matmul_mx(
                 out=bank[:],
@@ -151,8 +151,8 @@ def tile_list_parcel_conflict_scorer_kernel(
         def quantise_w1(g, a, raw):
             w16 = six.tile([P, KP * PACK], BF16, name="w1_16", tag="w16", align_bytes=64)
             nc.scalar.copy(
-                out=w16[:].rearrange("p (t m i) -> p m i t", t=PACK, i=PACK),
-                in_=raw[:].rearrange("p i (m t) -> p m i t", t=PACK),
+                out=w16[:].rearrange("p (h e m i) -> p h m i e", h=2, e=2, i=PACK),
+                in_=raw[:].rearrange("p i (m h e) -> p h m i e", h=2, e=2),
             )
             nc.vector.quantize_mx(out=w1_c[g][a][:].bitcast(FP8X4), scales=w1_sc[g][a][:], in_=w16[:])
 
@@ -195,7 +195,7 @@ def tile_list_parcel_conflict_scorer_kernel(
             place(0, t, b_first[:])
         deal_w2(1)
         for t in range(PACK):
-            if STG[t] < 0:
+            if STG[t] == -1:
                 b_first = quad.tile([P, PL], F32, name="b_first", tag="diff")
                 place(1, t, b_first[:])
         for g in range(GROUPS):
@@ -226,9 +226,13 @@ def tile_list_parcel_conflict_scorer_kernel(
         scales = kept([P, 2 * GROUPS * S], U8, "scales")
         result = big.tile([P, SLICES * S], F32, name="result", tag="big", align_bytes=64)
 
-        def cols_of(which, g, c):
-            start = 2 * (g * S + c * CHUNK) + which * CHUNK
-            return slice(start, start + CHUNK)
+        b_late = big.tile([P, PACK * PL], F32, name="b_late", tag="big", align_bytes=64)
+        for t in range(PACK):
+            if STG[t] == -2:
+                place(1, t, b_late[:, PL * t : PL * (t + 1)])
+
+        def code_col(which, g, u):
+            return (2 * (g * (S // UNIT) + u) + which) * UNIT
 
         units = [(g, u) for g in range(GROUPS) for u in range(S // UNIT)]
         per_chunk = CHUNK // UNIT
@@ -242,16 +246,14 @@ def tile_list_parcel_conflict_scorer_kernel(
         def paired(ap3):
             return ap3.rearrange("p t (c e) -> p c t e", e=2)
 
-        def part(which, g, u):
-            first = (which * CHUNK + (u % per_chunk) * UNIT) * PACK
-            return az16[g, u // per_chunk][:, first : first + UNIT * PACK]
+        def part(which, g, u, count=1):
+            first = (2 * (u % per_chunk) + which) * UNIT * PACK
+            return az16[g, u // per_chunk][:, first : first + count * UNIT * PACK]
 
-        def quantise(first, count, g, c):
-            cols = slice(cols_of(first, g, c).start, cols_of(first + count - 1, g, c).stop)
+        def quantise(which, g, u, count):
+            cols = slice(code_col(which, g, u), code_col(which, g, u) + count * UNIT)
             nc.vector.quantize_mx(
-                out=codes[:, cols].bitcast(FP8X4),
-                scales=scales[:, cols],
-                in_=az16[g, c][:, first * CHUNK * PACK : (first + count) * CHUNK * PACK],
+                out=codes[:, cols].bitcast(FP8X4), scales=scales[:, cols], in_=part(which, g, u, count)
             )
 
         def product(k):
@@ -321,42 +323,48 @@ def tile_list_parcel_conflict_scorer_kernel(
                 ALU.add,
             )
 
-        def scores(which, weights, weight_scales, c, s):
-            bank = psum.tile([P, CHUNK], F32, name="score_ps", tag="late" if which == 0 else YTAG)
-            for g in range(GROUPS):
-                nc.tensor.matmul_mx(
-                    out=bank[:],
-                    lhsT=weights(g)[:, P * s : P * (s + 1)].bitcast(FP8X4),
-                    lhsT_scale=weight_scales(g)[:, P * s : P * (s + 1)],
-                    rhs=codes[:, cols_of(which, g, c)].bitcast(FP8X4),
-                    rhs_scale=scales[:, cols_of(which, g, c)],
-                    start=(g == 0),
-                    stop=(g == GROUPS - 1),
-                )
+        def scores(which, weights, weight_scales, u):
+            bank = psum.tile([P, SLICES, UNIT], F32, name="score_ps", tag="late" if which == 0 else YTAG)
+            for s in range(SLICES):
+                for g in range(GROUPS):
+                    first = code_col(which, g, u)
+                    nc.tensor.matmul_mx(
+                        out=bank[:, s, :],
+                        lhsT=weights(g)[:, P * s : P * (s + 1)].bitcast(FP8X4),
+                        lhsT_scale=weight_scales(g)[:, P * s : P * (s + 1)],
+                        rhs=codes[:, first : first + UNIT].bitcast(FP8X4),
+                        rhs_scale=scales[:, first : first + UNIT],
+                        start=(g == 0),
+                        stop=(g == GROUPS - 1),
+                    )
             return bank
 
         skip_sb = {}
 
-        def finish_skip(c):
-            tile = pair.tile([P, SLICES, CHUNK], F32, name="skip_sb")
-            for s in range(SLICES):
-                bank = scores(0, lambda g: w5_c[g][:], lambda g: w5_sc[g][:], c, s)
-                nc.scalar.copy(out=tile[:, s, :], in_=bank[:])
-            skip_sb[c] = tile
+        def finish_skip(u):
+            bank = scores(0, lambda g: w5_c[g][:], lambda g: w5_sc[g][:], u)
+            skip_sb[u] = quad.tile([P, SLICES, UNIT], F32, name="skip_sb")
+            nc.scalar.copy(out=skip_sb[u][:], in_=bank[:])
 
-        def finish(c):
-            res = result[:, c * SLICES * CHUNK : (c + 1) * SLICES * CHUNK].rearrange("p (s j) -> p s j", s=SLICES)
-            for s in range(SLICES):
-                bank = scores(1, lambda g: w4_c[:, g, :], lambda g: w4_sc[PACK * g : P, :], c, s)
-                nc.vector.tensor_tensor(res[:, s, :], bank[:], skip_sb[c][:, s, :], ALU.min)
-            nc.sync.dma_start(
-                out=out[:, c * CHUNK : (c + 1) * CHUNK].rearrange("(s p) j -> p s j", p=P), in_=res
-            )
+        def staged_result(first, count):
+            res = result[:, first * SLICES * UNIT : (first + count) * SLICES * UNIT]
+            return res.rearrange("p (s j) -> p s j", s=SLICES)
 
-        def chunk_end(k):
-            return 0 <= k < len(units) and units[k][1] % per_chunk == per_chunk - 1
+        def finish(u):
+            bank = scores(1, lambda g: w4_c[:, g, :], lambda g: w4_sc[PACK * g : P, :], u)
+            if u >= S // UNIT - per_chunk:
+                res = staged_result(u, 1)
+            else:
+                i = u % per_chunk
+                res = staged_result(u - i, per_chunk)[:, :, i * UNIT : (i + 1) * UNIT]
+            nc.vector.tensor_tensor(res, bank[:], skip_sb[u][:], ALU.min)
 
-        for step in range(len(units) + 5):
+        def store(first, count):
+            cols = slice(first * UNIT, (first + count) * UNIT)
+            nc.sync.dma_start(out=out[:, cols].rearrange("(s p) j -> p s j", p=P), in_=staged_result(first, count))
+
+        final = len(units) - 1
+        for step in range(len(units) + 3):
             if step < len(units):
                 product(step)
             if turned(step - 1):
@@ -365,17 +373,23 @@ def tile_list_parcel_conflict_scorer_kernel(
                 gather(1, HELD[step - 1])
             if turned(step - 2):
                 turn_back(step - 2)
-            if chunk_end(step - 1) and units[step - 1][0] == GROUPS - 1:
-                quantise(0, 1, GROUPS - 1, units[step - 1][1] // per_chunk)
-                finish_skip(units[step - 1][1] // per_chunk)
             if 0 <= step - 2 < len(units):
                 add_marks(step - 2)
             if step in W5S:
                 quantise_w5(W5S.index(step), w5_later[W5S.index(step)])
-            if chunk_end(step - 3):
+            if step >= 3:
                 g, u = units[step - 3]
                 if g == GROUPS - 1:
-                    quantise(1, 1, g, u // per_chunk)
-                    finish(u // per_chunk)
-                else:
-                    quantise(0, 2, g, u // per_chunk)
+                    if step - 3 >= final - SPLIT:
+                        quantise(0, g, u, 1)
+                        quantise(1, g, u, 1)
+                    else:
+                        quantise(0, g, u, 2)
+                    finish_skip(u)
+                    finish(u)
+                    if u % per_chunk == per_chunk - 1 and step - 3 != final:
+                        store(u - per_chunk + 1, per_chunk)
+                    elif step - 3 >= final - 1:
+                        store(u, 1)
+                elif u % per_chunk == per_chunk - 1:
+                    quantise(0, g, u - per_chunk + 1, 2 * per_chunk)

@@ -18,20 +18,21 @@ ALU = mybir.AluOpType
 ACT = mybir.ActivationFunctionType
 
 P = 128
+QUADS, QUAD = 4, 32
 PACK = 4
 KP = P * PACK
 PASSES = K // KP
 GROUPS = H // KP
-HALF = 512
-CHUNK = 256
+HALF = S // 2
 UNIT = 128
-SLICES = N // P
-YTAG = "turn_ps"
-HELD = [0,1]
-SPLIT = -1
-W5S = [4,7]
-STG = [-1,-2,0,2]
-TRN = [0,1,2,3,4,5,6,7]
+UNITS = S // UNIT
+PAIR = 2
+OUT_TILES = N // P
+A_PART, Z_PART = 0, 1
+
+HELD_PASS = 1
+PLACE_AFTER = {0: 2, 2: 3}
+W5_AT = {4: 0, 7: 1}
 
 
 def tile_list_parcel_conflict_scorer_kernel(
@@ -41,56 +42,70 @@ def tile_list_parcel_conflict_scorer_kernel(
     nc = tc.nc
     with ExitStack() as ctx:
         keep = ctx.enter_context(tc.tile_pool(name="keep", bufs=1))
-        big = ctx.enter_context(tc.tile_pool(name="big", bufs=3))
+        big = ctx.enter_context(tc.tile_pool(name="big", bufs=6))
         quad = ctx.enter_context(tc.tile_pool(name="quad", bufs=4))
         six = ctx.enter_context(tc.tile_pool(name="six", bufs=6))
-        pair = ctx.enter_context(tc.tile_pool(name="pair", bufs=2))
         psum = ctx.enter_context(tc.psum_pool(name="psum", bufs=2))
 
-        def kept(shape, dtype, name):
-            return keep.tile(shape, dtype, name=name, align_bytes=64)
+        def kept(shape, dtype, name, tag=None):
+            return keep.tile(shape, dtype, name=name, tag=tag or name, align_bytes=64)
+
+        def large(shape, dtype, name):
+            return big.tile(shape, dtype, name=name, tag="big", align_bytes=64)
 
         offs_sb = keep.tile([P, S // 16], U16, name="offs_sb")
         offs2_sb = keep.tile([P, PL // 16], U16, name="offs2_sb")
         pos_sb = keep.tile([P, PL // 16], U16, name="pos_sb")
 
+        blocks = PL // P
         tab2_sc = kept([P, T3], U8, "tab2_sc")
         tab_sc = kept([P, T], U8, "tab_sc")
-        w2_sc_raw = kept([P, H], U8, "w2_sc_raw")
+        wgs_raw = large([P, PL], F32, "wgs_raw")
+        w2_raw = large([P, 2 * H], U8, "w2_raw")
+        tab2_w = large([P, T3], I32, "tab2_w")
+        wgs_turned = [large([P, 2, blocks, P], F32, "wgs_turned") for half in range(2)]
+        w2_sc_raw = large([P, H], U8, "w2_sc_raw")
         w4_sc = kept([P, N], U8, "w4_sc")
-        nc.vector.memset(tab2_sc[:].bitcast(I32), 0)
-        nc.vector.memset(w2_sc_raw[:].bitcast(I32), 0)
-        nc.vector.memset(tab_sc[:].bitcast(I32), 0)
-        nc.vector.memset(w4_sc[:].bitcast(I32), 0)
+        for scale_tile in (tab2_sc, w2_sc_raw, tab_sc, w4_sc):
+            nc.vector.memset(scale_tile[:].bitcast(I32), 0)
         ident = kept([P, P], F32, "ident")
         make_identity(nc, ident[:])
 
-        def load_scales(queue, tile, src):
+        def load_scales(scale_tile, src):
             rows = PACK * src.shape[0]
-            for q in range(4):
-                queue.dma_start(
-                    out=tile[32 * q : 32 * q + rows, :].bitcast(I32),
-                    in_=src[:, 4 * q : 4 * q + 4, :].bitcast(I32),
+            for q in range(QUADS):
+                nc.sync.dma_start(
+                    out=scale_tile[QUAD * q : QUAD * q + rows, :].bitcast(I32),
+                    in_=src[:, PACK * q : PACK * (q + 1), :].bitcast(I32),
                 )
 
-        tab2_w = six.tile([P, T3], I32, name="tab2_w", tag="stream", align_bytes=64)
-        w2_raw = kept([P, 2 * H], U8, "w2_raw")
         gain_sb = kept([P, GROUPS, PACK], F32, "gain_sb")
         nc.sync.dma_start(offs2_sb[:], offs2)
         nc.sync.dma_start(pos_sb[:], pos1)
         nc.sync.dma_start(out=gain_sb[:], in_=gain.rearrange("(g p t) -> p g t", g=GROUPS, t=PACK))
-        nc.sync.dma_start(offs_sb[:], offs)
+        nc.sync.dma_start(out=wgs_raw[:], in_=wgs)
         nc.sync.dma_start(out=w2_raw[:].bitcast(I32), in_=w2_words[0].bitcast(I32))
         nc.sync.dma_start(out=tab2_w[:], in_=tab2_words[0].rearrange("p t i -> p (t i)").bitcast(I32))
-        load_scales(nc.sync, tab2_sc, tab2_scales)
-        load_scales(nc.sync, w2_sc_raw, w2_scales)
-        wgs_sb = kept([P, PACK * PL], F32, "wgs_sb")
-        for q in range(4):
-            nc.sync.dma_start(
-                out=wgs_sb[32 * q : 32 * q + 32, :], in_=wgs.rearrange("(p t) m -> p (t m)", t=PACK)
-            )
-        pages = [[kept([P, S], F32, f"page{g}{t}") for t in range(PACK)] for g in range(GROUPS)]
+        load_scales(tab2_sc, tab2_scales)
+        load_scales(w2_sc_raw, w2_scales)
 
+        wgs_sb = kept([P, PACK * PL], F32, "wgs_sb")
+        bank = psum.tile([P, blocks, P], F32, name="turn_ps")
+        for block in range(blocks):
+            nc.tensor.transpose(bank[:, block, :], wgs_raw[:, P * block : P * (block + 1)], ident[:])
+        for half in range(2):
+            for q in range(QUADS):
+                nc.scalar.copy(
+                    out=wgs_turned[half][:, :, :, QUAD * q : QUAD * (q + 1)],
+                    in_=bank[:].rearrange("p b (m h e) -> p h e b m", h=2, e=2)[:, half],
+                )
+        for t in range(PACK):
+            bank = psum.tile([P, blocks, P], F32, name="back_ps")
+            for block in range(blocks):
+                nc.tensor.transpose(bank[:, block, :], wgs_turned[t // 2][:, t % 2, block, :], ident[:])
+            nc.scalar.copy(out=wgs_sb[:, PL * t : PL * (t + 1)], in_=bank[:].rearrange("p b m -> p (b m)"))
+
+        pages = [[kept([P, S], F32, f"page{g}{t}") for t in range(PACK)] for g in range(GROUPS)]
         w2_c = kept([P, 2 * H], U8, "w2_c")
         w2_sc = kept([P, H], U8, "w2_sc")
         v2 = kept([P, PL], U32, "v2")
@@ -110,13 +125,13 @@ def tile_list_parcel_conflict_scorer_kernel(
             )
 
         def place(g, t, b_sb):
-            s = PACK * g + t
+            first = KP * g + P * t
             nc.vector.memset(pages[g][t][:].bitcast(I32), 0)
             bank = psum.tile([P, PL], F32, name="b_ps", tag="late")
             nc.tensor.matmul_mx(
                 out=bank[:],
-                lhsT=w2_c[:, 2 * P * s : 2 * P * (s + 1)].bitcast(FP4X4),
-                lhsT_scale=w2_sc[:, P * s : P * (s + 1)],
+                lhsT=w2_c[:, 2 * first : 2 * (first + P)].bitcast(FP4X4),
+                lhsT_scale=w2_sc[:, first : first + P],
                 rhs=v2[:].bitcast(FP8X4),
                 rhs_scale=v2_sc[:],
                 start=True,
@@ -134,45 +149,30 @@ def tile_list_parcel_conflict_scorer_kernel(
             return offs_sb[:, h * HALF // 16 : (h + 1) * HALF // 16]
 
         def gather(h, a):
-            v[h, a] = keep.tile([P, HALF], U32, name="v", tag=f"v{h}{a}", align_bytes=64)
+            v[h, a] = kept([P, HALF], U32, "v", tag=f"v{h}{a}")
             nc.vector.tensor_copy(v[h, a][:], tab_w[a][:].bitcast(U32).indirect(entries(h)))
 
         w1_c = [[kept([P, KP], U32, f"w1_c{g}{a}") for a in range(PASSES)] for g in range(GROUPS)]
         w1_sc = [[kept([P, KP], U8, f"w1_sc{g}{a}") for a in range(PASSES)] for g in range(GROUPS)]
 
-        def load_w1(g, a):
-            raw = six.tile([P, PACK, KP], F32, name="w1_raw", tag="stream", align_bytes=64)
-            nc.sync.dma_start(
-                out=raw[:],
-                in_=w1[KP * a : KP * (a + 1), KP * g : KP * (g + 1)].rearrange("(p i) c -> p i c", i=PACK),
-            )
-            return raw
-
         def quantise_w1(g, a, raw):
             w16 = six.tile([P, KP * PACK], BF16, name="w1_16", tag="w16", align_bytes=64)
             nc.scalar.copy(
                 out=w16[:].rearrange("p (h e m i) -> p h m i e", h=2, e=2, i=PACK),
-                in_=raw[:].rearrange("p i (m h e) -> p h m i e", h=2, e=2),
+                in_=raw[:, :, KP * g : KP * (g + 1)].rearrange("p i (m h e) -> p h m i e", h=2, e=2),
             )
             nc.vector.quantize_mx(out=w1_c[g][a][:].bitcast(FP8X4), scales=w1_sc[g][a][:], in_=w16[:])
 
         w5_c = [kept([P, N], U32, f"w5_c{g}") for g in range(GROUPS)]
         w5_sc = [kept([P, N], U8, f"w5_sc{g}") for g in range(GROUPS)]
 
-        def load_w5(g):
-            raw = six.tile([P, PACK, N], F32, name="w5_raw", tag="stream", align_bytes=64)
-            nc.sync.dma_start(
-                out=raw[:], in_=w5[KP * g : KP * (g + 1), :].rearrange("(p i) c -> p i c", i=PACK)
-            )
-            return raw
-
-        def quantise_w5(g, raw):
+        def quantise_w5(g):
             w16 = six.tile([P, N * PACK], BF16, name="w5_16", tag="w16", align_bytes=64)
             nc.scalar.copy(
                 out=w16[:].rearrange("p (c e i) -> p c i e", e=2, i=PACK),
-                in_=raw[:].rearrange("p i (c e) -> p c i e", e=2),
+                in_=w5_raw[:, g].rearrange("p i (c e) -> p c i e", e=2),
             )
-            for c0, c1 in ((0, 256), (256, N)):
+            for c0, c1 in ((0, 2 * P), (2 * P, N)):
                 nc.vector.quantize_mx(
                     out=w5_c[g][:, c0:c1].bitcast(FP8X4),
                     scales=w5_sc[g][:, c0:c1],
@@ -181,83 +181,65 @@ def tile_list_parcel_conflict_scorer_kernel(
 
         marks_sb = {}
 
-        def load_marks(g, h):
-            tile = six.tile([P, PACK, HALF], F32, name="marks_sb", tag="stream", align_bytes=64)
+        def load_marks(g):
+            marks_sb[g] = large([P, PACK, S], F32, "marks_sb")
             nc.sync.dma_start(
-                out=tile[:],
-                in_=marks[KP * g : KP * (g + 1), HALF * h : HALF * (h + 1)].rearrange("(p t) j -> p t j", t=PACK),
+                out=marks_sb[g][:], in_=marks[KP * g : KP * (g + 1), :].rearrange("(p t) j -> p t j", t=PACK)
             )
-            marks_sb[g, h] = tile
 
         deal_w2(0)
         for t in range(PACK):
-            b_first = quad.tile([P, PL], F32, name="b_first", tag="a32")
-            place(0, t, b_first[:])
+            b_sb = quad.tile([P, PL], F32, name="b_sb", tag="a32")
+            place(0, t, b_sb[:])
         deal_w2(1)
-        for t in range(PACK):
-            if STG[t] == -1:
-                b_first = quad.tile([P, PL], F32, name="b_first", tag="diff")
-                place(1, t, b_first[:])
-        for g in range(GROUPS):
-            for a in range(PASSES):
-                quantise_w1(g, a, load_w1(g, a))
-        load_scales(nc.sync, tab_sc, tab_scales)
-        tab_w = []
+        place(1, 0, kept([P, PL], F32, "b_sb", tag="w4_c")[:])
         for a in range(PASSES):
-            tile = big.tile([P, T], I32, name=f"tab_w{a}", tag="big", align_bytes=64)
-            nc.sync.dma_start(out=tile[:], in_=tab_words[a].rearrange("p t i -> p (t i)").bitcast(I32))
-            tab_w.append(tile)
+            w1_raw = large([P, PACK, H], F32, "w1_raw")
+            nc.sync.dma_start(
+                out=w1_raw[:], in_=w1[KP * a : KP * (a + 1), :].rearrange("(p i) c -> p i c", i=PACK)
+            )
+            for g in range(GROUPS):
+                quantise_w1(g, a, w1_raw)
+        nc.sync.dma_start(offs_sb[:], offs)
+        load_scales(tab_sc, tab_scales)
+        tab_w = [large([P, T], I32, f"tab_w{a}") for a in range(PASSES)]
+        for a in range(PASSES):
+            nc.sync.dma_start(out=tab_w[a][:], in_=tab_words[a].rearrange("p t i -> p (t i)").bitcast(I32))
         for h in range(S // HALF):
             nc.vector.tensor_copy(v_sc[h][:], tab_sc[:].indirect(entries(h)))
         for a in range(PASSES):
             gather(0, a)
-            if a not in HELD:
+            if a != HELD_PASS:
                 gather(1, a)
-        load_marks(0, 0)
-        w5_later = [load_w5(g) for g in range(GROUPS)]
-        load_marks(0, 1)
-        load_scales(nc.sync, w4_sc, w4_scales)
+        load_marks(0)
+        w5_raw = large([P, GROUPS, PACK, N], F32, "w5_raw")
+        nc.sync.dma_start(out=w5_raw[:], in_=w5.rearrange("(g p i) c -> p g i c", g=GROUPS, i=PACK))
+        load_scales(w4_sc, w4_scales)
         w4_c = kept([P, GROUPS, N], I32, "w4_c")
         nc.sync.dma_start(out=w4_c[:], in_=w4_words.rearrange("a p c i -> p a (c i)").bitcast(I32))
-        load_marks(1, 0)
-        load_marks(1, 1)
+        load_marks(1)
 
-        codes = big.tile([P, 2 * GROUPS * S], U32, name="codes", tag="big", align_bytes=64)
+        codes = large([P, 2 * GROUPS * S], U32, "codes")
         scales = kept([P, 2 * GROUPS * S], U8, "scales")
-        result = big.tile([P, SLICES * S], F32, name="result", tag="big", align_bytes=64)
+        result = large([P, OUT_TILES * S], F32, "result")
+        place(1, 1, large([P, PL], F32, "b_sb")[:])
 
-        b_late = big.tile([P, PACK * PL], F32, name="b_late", tag="big", align_bytes=64)
-        for t in range(PACK):
-            if STG[t] == -2:
-                place(1, t, b_late[:, PL * t : PL * (t + 1)])
+        az16, a_neg, diff, skip_sb = {}, {}, {}, {}
 
-        def code_col(which, g, u):
-            return (2 * (g * (S // UNIT) + u) + which) * UNIT
+        def code_col(part, g, u):
+            return (2 * (g * UNITS + u) + part) * UNIT
 
-        units = [(g, u) for g in range(GROUPS) for u in range(S // UNIT)]
-        per_chunk = CHUNK // UNIT
-        az16, diff, a32 = {}, {}, {}
+        def values(part, g, u, parts=1):
+            first = (2 * (u % PAIR) + part) * UNIT * PACK
+            return az16[g, u // PAIR][:, first : first + parts * UNIT * PACK]
 
-        staged = STG
-
-        def turned(k):
-            return k in TRN
-
-        def paired(ap3):
-            return ap3.rearrange("p t (c e) -> p c t e", e=2)
-
-        def part(which, g, u, count=1):
-            first = (2 * (u % per_chunk) + which) * UNIT * PACK
-            return az16[g, u // per_chunk][:, first : first + count * UNIT * PACK]
-
-        def quantise(which, g, u, count):
-            cols = slice(code_col(which, g, u), code_col(which, g, u) + count * UNIT)
+        def quantise(g, u, count):
+            cols = slice(code_col(A_PART, g, u), code_col(A_PART, g, u + count))
             nc.vector.quantize_mx(
-                out=codes[:, cols].bitcast(FP8X4), scales=scales[:, cols], in_=part(which, g, u, count)
+                out=codes[:, cols].bitcast(FP8X4), scales=scales[:, cols], in_=values(A_PART, g, u, 2 * count)
             )
 
-        def product(k):
-            g, u = units[k]
+        def product(g, u):
             h, j0 = divmod(u * UNIT, HALF)
             bank = psum.tile([P, PACK, UNIT], F32, name="a_ps", tag="a")
             for t in range(PACK):
@@ -271,67 +253,67 @@ def tile_list_parcel_conflict_scorer_kernel(
                         start=(a == 0),
                         stop=(a == PASSES - 1),
                     )
-            if u % per_chunk == 0:
-                az16[g, u // per_chunk] = six.tile([P, 2 * CHUNK * PACK], BF16, name="az16", tag="w16", align_bytes=64)
-            if turned(k):
-                if k < len(HELD):
-                    a32[k] = keep.tile([P, PACK, UNIT], F32, name="a32", tag=f"v1{HELD[k]}", align_bytes=64)
+            if u % PAIR == 0:
+                az16[g, u // PAIR] = six.tile(
+                    [P, 2 * PAIR * UNIT * PACK], BF16, name="az16", tag="w16", align_bytes=64
+                )
+            if g == 0:
+                if u == 0:
+                    a_neg[u] = kept([P, PACK, UNIT], F32, "a_neg", tag=f"v1{HELD_PASS}")
                 else:
-                    a32[k] = quad.tile([P, PACK, UNIT], F32, name="a32", tag="a32")
-                nc.scalar.activation(out=a32[k][:], in_=bank[:], func=ACT.Copy, scale=-1.0)
+                    a_neg[u] = quad.tile([P, PACK, UNIT], F32, name="a_neg", tag="a32")
+                nc.scalar.activation(out=a_neg[u][:], in_=bank[:], func=ACT.Copy, scale=-1.0)
             else:
-                diff[k] = quad.tile([P, PACK, UNIT], F32, name="diff")
+                diff[g, u] = quad.tile([P, PACK, UNIT], F32, name="diff")
                 for t in range(PACK):
                     nc.vector.tensor_tensor(
-                        diff[k][:, t, :], bank[:, t, :], pages[g][t][:, u * UNIT : (u + 1) * UNIT], ALU.subtract
+                        diff[g, u][:, t, :], bank[:, t, :], pages[g][t][:, u * UNIT : (u + 1) * UNIT], ALU.subtract
                     )
-                nc.scalar.activation(out=diff[k][:], in_=diff[k][:], func=ACT.Abs)
+                nc.scalar.activation(out=diff[g, u][:], in_=diff[g, u][:], func=ACT.Abs)
             nc.scalar.copy(
-                out=part(0, g, u).rearrange("p (n t) -> p n t", t=PACK), in_=bank[:].rearrange("p t n -> p n t")
+                out=values(A_PART, g, u).rearrange("p (n t) -> p n t", t=PACK),
+                in_=bank[:].rearrange("p t n -> p n t"),
             )
 
-        def turn(k):
-            g, u = units[k]
+        def turn(u):
             bank = psum.tile([P, PACK, P], F32, name="turn_ps")
             for t in range(PACK):
                 nc.tensor.matmul(
-                    out=bank[:, t, :], lhsT=pages[g][t][:, u * UNIT : (u + 1) * UNIT], rhs=ident[:],
+                    out=bank[:, t, :], lhsT=a_neg[u][:, t, :], rhs=ident[:],
                     is_transpose=True, start=True, stop=False,
                 )
                 nc.tensor.matmul(
-                    out=bank[:, t, :], lhsT=a32[k][:, t, :], rhs=ident[:],
+                    out=bank[:, t, :], lhsT=pages[0][t][:, u * UNIT : (u + 1) * UNIT], rhs=ident[:],
                     is_transpose=True, start=False, stop=True,
                 )
-            diff[k] = quad.tile([P, PACK, UNIT], F32, name="diff")
-            nc.scalar.activation(out=diff[k][:], in_=bank[:], func=ACT.Abs)
+            diff[0, u] = quad.tile([P, PACK, UNIT], F32, name="diff")
+            nc.scalar.activation(out=diff[0, u][:], in_=bank[:], func=ACT.Abs)
 
-        def turn_back(k):
+        def turn_back(u):
             bank = psum.tile([P, PACK, UNIT], F32, name="back_ps")
             for t in range(PACK):
-                nc.tensor.transpose(bank[:, t, :], diff[k][:, t, :], ident[:])
-            if k in staged:
-                place(1, staged.index(k), diff[k][:].rearrange("p t n -> p (t n)"))
-            diff[k] = bank
+                nc.tensor.transpose(bank[:, t, :], diff[0, u][:, t, :], ident[:])
+            if u in PLACE_AFTER:
+                place(1, PLACE_AFTER[u], diff[0, u][:].rearrange("p t n -> p (t n)"))
+            diff[0, u] = bank
 
-        def add_marks(k):
-            g, u = units[k]
-            h, j0 = divmod(u * UNIT, HALF)
+        def add_marks(g, u):
             nc.vector.tensor_tensor(
-                part(1, g, u).rearrange("p (c e t) -> p c t e", e=2, t=PACK),
-                paired(diff[k][:]),
-                paired(marks_sb[g, h][:, :, j0 : j0 + UNIT]),
+                values(Z_PART, g, u).rearrange("p (c e t) -> p c t e", e=2, t=PACK),
+                diff[g, u][:].rearrange("p t (c e) -> p c t e", e=2),
+                marks_sb[g][:, :, u * UNIT : (u + 1) * UNIT].rearrange("p t (c e) -> p c t e", e=2),
                 ALU.add,
             )
 
-        def scores(which, weights, weight_scales, u):
-            bank = psum.tile([P, SLICES, UNIT], F32, name="score_ps", tag="late" if which == 0 else YTAG)
-            for s in range(SLICES):
+        def scores(part, weights, weight_scales, u, tag):
+            bank = psum.tile([P, OUT_TILES, UNIT], F32, name="score_ps", tag=tag)
+            for s in range(OUT_TILES):
                 for g in range(GROUPS):
-                    first = code_col(which, g, u)
+                    first = code_col(part, g, u)
                     nc.tensor.matmul_mx(
                         out=bank[:, s, :],
-                        lhsT=weights(g)[:, P * s : P * (s + 1)].bitcast(FP8X4),
-                        lhsT_scale=weight_scales(g)[:, P * s : P * (s + 1)],
+                        lhsT=weights[g][:, P * s : P * (s + 1)].bitcast(FP8X4),
+                        lhsT_scale=weight_scales[g][:, P * s : P * (s + 1)],
                         rhs=codes[:, first : first + UNIT].bitcast(FP8X4),
                         rhs_scale=scales[:, first : first + UNIT],
                         start=(g == 0),
@@ -339,57 +321,43 @@ def tile_list_parcel_conflict_scorer_kernel(
                     )
             return bank
 
-        skip_sb = {}
-
-        def finish_skip(u):
-            bank = scores(0, lambda g: w5_c[g][:], lambda g: w5_sc[g][:], u)
-            skip_sb[u] = quad.tile([P, SLICES, UNIT], F32, name="skip_sb")
-            nc.scalar.copy(out=skip_sb[u][:], in_=bank[:])
-
-        def staged_result(first, count):
-            res = result[:, first * SLICES * UNIT : (first + count) * SLICES * UNIT]
-            return res.rearrange("p (s j) -> p s j", s=SLICES)
-
         def finish(u):
-            bank = scores(1, lambda g: w4_c[:, g, :], lambda g: w4_sc[PACK * g : P, :], u)
-            if u >= S // UNIT - per_chunk:
-                res = staged_result(u, 1)
-            else:
-                i = u % per_chunk
-                res = staged_result(u - i, per_chunk)[:, :, i * UNIT : (i + 1) * UNIT]
-            nc.vector.tensor_tensor(res, bank[:], skip_sb[u][:], ALU.min)
+            bank = scores(A_PART, [c[:] for c in w5_c], [c[:] for c in w5_sc], u, "late")
+            skip_sb[u] = quad.tile([P, OUT_TILES, UNIT], F32, name="skip_sb")
+            nc.scalar.copy(out=skip_sb[u][:], in_=bank[:])
+            bank = scores(
+                Z_PART, [w4_c[:, g, :] for g in range(GROUPS)], [w4_sc[PACK * g : P, :] for g in range(GROUPS)],
+                u, "turn_ps",
+            )
+            count = 1 if u >= UNITS - PAIR else PAIR
+            first = u - u % count
+            staged = result[:, first * OUT_TILES * UNIT : (first + count) * OUT_TILES * UNIT]
+            staged = staged.rearrange("p (s j) -> p s j", s=OUT_TILES)
+            nc.vector.tensor_tensor(
+                staged[:, :, (u - first) * UNIT : (u - first + 1) * UNIT], bank[:], skip_sb[u][:], ALU.min
+            )
+            if u == first + count - 1:
+                cols = slice(first * UNIT, (first + count) * UNIT)
+                nc.sync.dma_start(out=out[:, cols].rearrange("(s p) j -> p s j", p=P), in_=staged)
 
-        def store(first, count):
-            cols = slice(first * UNIT, (first + count) * UNIT)
-            nc.sync.dma_start(out=out[:, cols].rearrange("(s p) j -> p s j", p=P), in_=staged_result(first, count))
-
-        final = len(units) - 1
-        for step in range(len(units) + 3):
-            if step < len(units):
-                product(step)
-            if turned(step - 1):
+        order = [(g, u) for g in range(GROUPS) for u in range(UNITS)]
+        for step in range(len(order) + 3):
+            if step < len(order):
+                product(*order[step])
+            if 0 <= step - 1 < UNITS:
                 turn(step - 1)
-            if 0 <= step - 1 < len(HELD):
-                gather(1, HELD[step - 1])
-            if turned(step - 2):
+            if step - 1 == 0:
+                gather(1, HELD_PASS)
+            if 0 <= step - 2 < UNITS:
                 turn_back(step - 2)
-            if 0 <= step - 2 < len(units):
-                add_marks(step - 2)
-            if step in W5S:
-                quantise_w5(W5S.index(step), w5_later[W5S.index(step)])
+            if 0 <= step - 2 < len(order):
+                add_marks(*order[step - 2])
+            if step in W5_AT:
+                quantise_w5(W5_AT[step])
             if step >= 3:
-                g, u = units[step - 3]
+                g, u = order[step - 3]
                 if g == GROUPS - 1:
-                    if step - 3 >= final - SPLIT:
-                        quantise(0, g, u, 1)
-                        quantise(1, g, u, 1)
-                    else:
-                        quantise(0, g, u, 2)
-                    finish_skip(u)
+                    quantise(g, u, 1)
                     finish(u)
-                    if u % per_chunk == per_chunk - 1 and step - 3 != final:
-                        store(u - per_chunk + 1, per_chunk)
-                    elif step - 3 >= final - 1:
-                        store(u, 1)
-                elif u % per_chunk == per_chunk - 1:
-                    quantise(0, g, u - per_chunk + 1, 2 * per_chunk)
+                elif u % PAIR == PAIR - 1:
+                    quantise(g, u - PAIR + 1, PAIR)

from contextlib import ExitStack

import concourse.mybir as mybir
from concourse.masks import make_identity

K, K2, H, N, T, T3, S, PL = 1536, 512, 1024, 384, 4096, 2048, 1024, 512
FLOPS = 2 * (K * H * S + K2 * H * PL + 2 * H * N * S)

F32 = mybir.dt.float32
BF16 = mybir.dt.bfloat16
I32 = mybir.dt.int32
U32 = mybir.dt.uint32
U16 = mybir.dt.uint16
U8 = mybir.dt.uint8
FP8X4 = mybir.dt.float8_e4m3fn_x4
FP4X4 = mybir.dt.float4_e2m1fn_x4
ALU = mybir.AluOpType
ACT = mybir.ActivationFunctionType

P = 128
QUADS, QUAD = 4, 32
PACK = 4
KP = P * PACK
PASSES = K // KP
GROUPS = H // KP
HALF = S // 2
UNIT = 128
UNITS = S // UNIT
PAIR = 2
OUT_TILES = N // P
A_PART, Z_PART = 0, 1

HELD_PASS = 1
PLACE_AFTER = {0: 2, 2: 3}
W5_AT = {4: 0, 7: 1}


def tile_list_parcel_conflict_scorer_kernel(
    tc, tab_words, tab_scales, tab2_words, tab2_scales, offs, offs2, pos1, w1,
    w2_words, w2_scales, gain, wgs, marks, w4_words, w4_scales, w5, out,
):
    nc = tc.nc
    with ExitStack() as ctx:
        keep = ctx.enter_context(tc.tile_pool(name="keep", bufs=1))
        big = ctx.enter_context(tc.tile_pool(name="big", bufs=6))
        quad = ctx.enter_context(tc.tile_pool(name="quad", bufs=4))
        six = ctx.enter_context(tc.tile_pool(name="six", bufs=6))
        psum = ctx.enter_context(tc.psum_pool(name="psum", bufs=2))

        def kept(shape, dtype, name, tag=None):
            return keep.tile(shape, dtype, name=name, tag=tag or name, align_bytes=64)

        def large(shape, dtype, name):
            return big.tile(shape, dtype, name=name, tag="big", align_bytes=64)

        offs_sb = keep.tile([P, S // 16], U16, name="offs_sb")
        offs2_sb = keep.tile([P, PL // 16], U16, name="offs2_sb")
        pos_sb = keep.tile([P, PL // 16], U16, name="pos_sb")

        blocks = PL // P
        tab2_sc = kept([P, T3], U8, "tab2_sc")
        tab_sc = kept([P, T], U8, "tab_sc")
        wgs_raw = large([P, PL], F32, "wgs_raw")
        w2_raw = large([P, 2 * H], U8, "w2_raw")
        tab2_w = large([P, T3], I32, "tab2_w")
        wgs_turned = [large([P, 2, blocks, P], F32, "wgs_turned") for half in range(2)]
        w2_sc_raw = large([P, H], U8, "w2_sc_raw")
        w4_sc = kept([P, N], U8, "w4_sc")
        for scale_tile in (tab2_sc, w2_sc_raw, tab_sc, w4_sc):
            nc.vector.memset(scale_tile[:].bitcast(I32), 0)
        ident = kept([P, P], F32, "ident")
        make_identity(nc, ident[:])

        def load_scales(scale_tile, src):
            rows = PACK * src.shape[0]
            for q in range(QUADS):
                nc.sync.dma_start(
                    out=scale_tile[QUAD * q : QUAD * q + rows, :].bitcast(I32),
                    in_=src[:, PACK * q : PACK * (q + 1), :].bitcast(I32),
                )

        gain_sb = kept([P, GROUPS, PACK], F32, "gain_sb")
        nc.sync.dma_start(offs2_sb[:], offs2)
        nc.sync.dma_start(pos_sb[:], pos1)
        nc.sync.dma_start(out=gain_sb[:], in_=gain.rearrange("(g p t) -> p g t", g=GROUPS, t=PACK))
        nc.sync.dma_start(out=wgs_raw[:], in_=wgs)
        nc.sync.dma_start(out=w2_raw[:].bitcast(I32), in_=w2_words[0].bitcast(I32))
        nc.sync.dma_start(out=tab2_w[:], in_=tab2_words[0].rearrange("p t i -> p (t i)").bitcast(I32))
        load_scales(tab2_sc, tab2_scales)
        load_scales(w2_sc_raw, w2_scales)

        wgs_sb = kept([P, PACK * PL], F32, "wgs_sb")
        bank = psum.tile([P, blocks, P], F32, name="turn_ps")
        for block in range(blocks):
            nc.tensor.transpose(bank[:, block, :], wgs_raw[:, P * block : P * (block + 1)], ident[:])
        for half in range(2):
            for q in range(QUADS):
                nc.scalar.copy(
                    out=wgs_turned[half][:, :, :, QUAD * q : QUAD * (q + 1)],
                    in_=bank[:].rearrange("p b (m h e) -> p h e b m", h=2, e=2)[:, half],
                )
        for t in range(PACK):
            bank = psum.tile([P, blocks, P], F32, name="back_ps")
            for block in range(blocks):
                nc.tensor.transpose(bank[:, block, :], wgs_turned[t // 2][:, t % 2, block, :], ident[:])
            nc.scalar.copy(out=wgs_sb[:, PL * t : PL * (t + 1)], in_=bank[:].rearrange("p b m -> p (b m)"))

        pages = [[kept([P, S], F32, f"page{g}{t}") for t in range(PACK)] for g in range(GROUPS)]
        w2_c = kept([P, 2 * H], U8, "w2_c")
        w2_sc = kept([P, H], U8, "w2_sc")
        v2 = kept([P, PL], U32, "v2")
        v2_sc = kept([P, PL], U8, "v2_sc")
        nc.vector.tensor_copy(v2[:], tab2_w[:].bitcast(U32).indirect(offs2_sb[:]))
        nc.vector.tensor_copy(v2_sc[:], tab2_sc[:].indirect(offs2_sb[:]))

        def deal_w2(g):
            words, cols = slice(2 * KP * g, 2 * KP * (g + 1)), slice(KP * g, KP * (g + 1))
            nc.vector.tensor_copy(
                out=w2_c[:, words].rearrange("p (t m b) -> p t m b", t=PACK, b=2),
                in_=w2_raw[:, words].rearrange("p (m t b) -> p t m b", t=PACK, b=2),
            )
            nc.vector.tensor_copy(
                out=w2_sc[:, cols].rearrange("p (t m) -> p t m", t=PACK),
                in_=w2_sc_raw[:, cols].rearrange("p (m t) -> p t m", t=PACK),
            )

        def place(g, t, b_sb):
            first = KP * g + P * t
            nc.vector.memset(pages[g][t][:].bitcast(I32), 0)
            bank = psum.tile([P, PL], F32, name="b_ps", tag="late")
            nc.tensor.matmul_mx(
                out=bank[:],
                lhsT=w2_c[:, 2 * first : 2 * (first + P)].bitcast(FP4X4),
                lhsT_scale=w2_sc[:, first : first + P],
                rhs=v2[:].bitcast(FP8X4),
                rhs_scale=v2_sc[:],
                start=True,
                stop=True,
            )
            nc.scalar.activation(out=b_sb, in_=bank[:], func=ACT.Copy, scale=gain_sb[:, g, t : t + 1])
            nc.vector.tensor_tensor(
                pages[g][t][:].indirect(pos_sb[:]), b_sb, wgs_sb[:, PL * t : PL * (t + 1)], ALU.mult
            )

        v = {}
        v_sc = [kept([P, HALF], U8, f"v_sc{h}") for h in range(S // HALF)]

        def entries(h):
            return offs_sb[:, h * HALF // 16 : (h + 1) * HALF // 16]

        def gather(h, a):
            v[h, a] = kept([P, HALF], U32, "v", tag=f"v{h}{a}")
            nc.vector.tensor_copy(v[h, a][:], tab_w[a][:].bitcast(U32).indirect(entries(h)))

        w1_c = [[kept([P, KP], U32, f"w1_c{g}{a}") for a in range(PASSES)] for g in range(GROUPS)]
        w1_sc = [[kept([P, KP], U8, f"w1_sc{g}{a}") for a in range(PASSES)] for g in range(GROUPS)]

        def quantise_w1(g, a, raw):
            w16 = six.tile([P, KP * PACK], BF16, name="w1_16", tag="w16", align_bytes=64)
            nc.scalar.copy(
                out=w16[:].rearrange("p (h e m i) -> p h m i e", h=2, e=2, i=PACK),
                in_=raw[:, :, KP * g : KP * (g + 1)].rearrange("p i (m h e) -> p h m i e", h=2, e=2),
            )
            nc.vector.quantize_mx(out=w1_c[g][a][:].bitcast(FP8X4), scales=w1_sc[g][a][:], in_=w16[:])

        w5_c = [kept([P, N], U32, f"w5_c{g}") for g in range(GROUPS)]
        w5_sc = [kept([P, N], U8, f"w5_sc{g}") for g in range(GROUPS)]

        def quantise_w5(g):
            w16 = six.tile([P, N * PACK], BF16, name="w5_16", tag="w16", align_bytes=64)
            nc.scalar.copy(
                out=w16[:].rearrange("p (c e i) -> p c i e", e=2, i=PACK),
                in_=w5_raw[:, g].rearrange("p i (c e) -> p c i e", e=2),
            )
            for c0, c1 in ((0, 2 * P), (2 * P, N)):
                nc.vector.quantize_mx(
                    out=w5_c[g][:, c0:c1].bitcast(FP8X4),
                    scales=w5_sc[g][:, c0:c1],
                    in_=w16[:, PACK * c0 : PACK * c1],
                )

        marks_sb = {}

        def load_marks(g):
            marks_sb[g] = large([P, PACK, S], F32, "marks_sb")
            nc.sync.dma_start(
                out=marks_sb[g][:], in_=marks[KP * g : KP * (g + 1), :].rearrange("(p t) j -> p t j", t=PACK)
            )

        deal_w2(0)
        for t in range(PACK):
            b_sb = quad.tile([P, PL], F32, name="b_sb", tag="a32")
            place(0, t, b_sb[:])
        deal_w2(1)
        place(1, 0, kept([P, PL], F32, "b_sb", tag="w4_c")[:])
        for a in range(PASSES):
            w1_raw = large([P, PACK, H], F32, "w1_raw")
            nc.sync.dma_start(
                out=w1_raw[:], in_=w1[KP * a : KP * (a + 1), :].rearrange("(p i) c -> p i c", i=PACK)
            )
            for g in range(GROUPS):
                quantise_w1(g, a, w1_raw)
        nc.sync.dma_start(offs_sb[:], offs)
        load_scales(tab_sc, tab_scales)
        tab_w = [large([P, T], I32, f"tab_w{a}") for a in range(PASSES)]
        for a in range(PASSES):
            nc.sync.dma_start(out=tab_w[a][:], in_=tab_words[a].rearrange("p t i -> p (t i)").bitcast(I32))
        for h in range(S // HALF):
            nc.vector.tensor_copy(v_sc[h][:], tab_sc[:].indirect(entries(h)))
        for a in range(PASSES):
            gather(0, a)
            if a != HELD_PASS:
                gather(1, a)
        load_marks(0)
        w5_raw = large([P, GROUPS, PACK, N], F32, "w5_raw")
        nc.sync.dma_start(out=w5_raw[:], in_=w5.rearrange("(g p i) c -> p g i c", g=GROUPS, i=PACK))
        load_scales(w4_sc, w4_scales)
        w4_c = kept([P, GROUPS, N], I32, "w4_c")
        nc.sync.dma_start(out=w4_c[:], in_=w4_words.rearrange("a p c i -> p a (c i)").bitcast(I32))
        load_marks(1)

        codes = large([P, 2 * GROUPS * S], U32, "codes")
        scales = kept([P, 2 * GROUPS * S], U8, "scales")
        result = large([P, OUT_TILES * S], F32, "result")
        place(1, 1, large([P, PL], F32, "b_sb")[:])

        az16, a_neg, diff, skip_sb = {}, {}, {}, {}

        def code_col(part, g, u):
            return (2 * (g * UNITS + u) + part) * UNIT

        def values(part, g, u, parts=1):
            first = (2 * (u % PAIR) + part) * UNIT * PACK
            return az16[g, u // PAIR][:, first : first + parts * UNIT * PACK]

        def quantise(g, u, count):
            cols = slice(code_col(A_PART, g, u), code_col(A_PART, g, u + count))
            nc.vector.quantize_mx(
                out=codes[:, cols].bitcast(FP8X4), scales=scales[:, cols], in_=values(A_PART, g, u, 2 * count)
            )

        def product(g, u):
            h, j0 = divmod(u * UNIT, HALF)
            bank = psum.tile([P, PACK, UNIT], F32, name="a_ps", tag="a")
            for t in range(PACK):
                for a in range(PASSES):
                    nc.tensor.matmul_mx(
                        out=bank[:, t, :],
                        lhsT=w1_c[g][a][:, P * t : P * (t + 1)].bitcast(FP8X4),
                        lhsT_scale=w1_sc[g][a][:, P * t : P * (t + 1)],
                        rhs=v[h, a][:, j0 : j0 + UNIT].bitcast(FP8X4),
                        rhs_scale=v_sc[h][PACK * a : P, j0 : j0 + UNIT],
                        start=(a == 0),
                        stop=(a == PASSES - 1),
                    )
            if u % PAIR == 0:
                az16[g, u // PAIR] = six.tile(
                    [P, 2 * PAIR * UNIT * PACK], BF16, name="az16", tag="w16", align_bytes=64
                )
            if g == 0:
                if u == 0:
                    a_neg[u] = kept([P, PACK, UNIT], F32, "a_neg", tag=f"v1{HELD_PASS}")
                else:
                    a_neg[u] = quad.tile([P, PACK, UNIT], F32, name="a_neg", tag="a32")
                nc.scalar.activation(out=a_neg[u][:], in_=bank[:], func=ACT.Copy, scale=-1.0)
            else:
                diff[g, u] = quad.tile([P, PACK, UNIT], F32, name="diff")
                for t in range(PACK):
                    nc.vector.tensor_tensor(
                        diff[g, u][:, t, :], bank[:, t, :], pages[g][t][:, u * UNIT : (u + 1) * UNIT], ALU.subtract
                    )
                nc.scalar.activation(out=diff[g, u][:], in_=diff[g, u][:], func=ACT.Abs)
            nc.scalar.copy(
                out=values(A_PART, g, u).rearrange("p (n t) -> p n t", t=PACK),
                in_=bank[:].rearrange("p t n -> p n t"),
            )

        def turn(u):
            bank = psum.tile([P, PACK, P], F32, name="turn_ps")
            for t in range(PACK):
                nc.tensor.matmul(
                    out=bank[:, t, :], lhsT=a_neg[u][:, t, :], rhs=ident[:],
                    is_transpose=True, start=True, stop=False,
                )
                nc.tensor.matmul(
                    out=bank[:, t, :], lhsT=pages[0][t][:, u * UNIT : (u + 1) * UNIT], rhs=ident[:],
                    is_transpose=True, start=False, stop=True,
                )
            diff[0, u] = quad.tile([P, PACK, UNIT], F32, name="diff")
            nc.scalar.activation(out=diff[0, u][:], in_=bank[:], func=ACT.Abs)

        def turn_back(u):
            bank = psum.tile([P, PACK, UNIT], F32, name="back_ps")
            for t in range(PACK):
                nc.tensor.transpose(bank[:, t, :], diff[0, u][:, t, :], ident[:])
            if u in PLACE_AFTER:
                place(1, PLACE_AFTER[u], diff[0, u][:].rearrange("p t n -> p (t n)"))
            diff[0, u] = bank

        def add_marks(g, u):
            nc.vector.tensor_tensor(
                values(Z_PART, g, u).rearrange("p (c e t) -> p c t e", e=2, t=PACK),
                diff[g, u][:].rearrange("p t (c e) -> p c t e", e=2),
                marks_sb[g][:, :, u * UNIT : (u + 1) * UNIT].rearrange("p t (c e) -> p c t e", e=2),
                ALU.add,
            )

        def scores(part, weights, weight_scales, u, tag):
            bank = psum.tile([P, OUT_TILES, UNIT], F32, name="score_ps", tag=tag)
            for s in range(OUT_TILES):
                for g in range(GROUPS):
                    first = code_col(part, g, u)
                    nc.tensor.matmul_mx(
                        out=bank[:, s, :],
                        lhsT=weights[g][:, P * s : P * (s + 1)].bitcast(FP8X4),
                        lhsT_scale=weight_scales[g][:, P * s : P * (s + 1)],
                        rhs=codes[:, first : first + UNIT].bitcast(FP8X4),
                        rhs_scale=scales[:, first : first + UNIT],
                        start=(g == 0),
                        stop=(g == GROUPS - 1),
                    )
            return bank

        def finish(u):
            bank = scores(A_PART, [c[:] for c in w5_c], [c[:] for c in w5_sc], u, "late")
            skip_sb[u] = quad.tile([P, OUT_TILES, UNIT], F32, name="skip_sb")
            nc.scalar.copy(out=skip_sb[u][:], in_=bank[:])
            bank = scores(
                Z_PART, [w4_c[:, g, :] for g in range(GROUPS)], [w4_sc[PACK * g : P, :] for g in range(GROUPS)],
                u, "turn_ps",
            )
            count = 1 if u >= UNITS - PAIR else PAIR
            first = u - u % count
            staged = result[:, first * OUT_TILES * UNIT : (first + count) * OUT_TILES * UNIT]
            staged = staged.rearrange("p (s j) -> p s j", s=OUT_TILES)
            nc.vector.tensor_tensor(
                staged[:, :, (u - first) * UNIT : (u - first + 1) * UNIT], bank[:], skip_sb[u][:], ALU.min
            )
            if u == first + count - 1:
                cols = slice(first * UNIT, (first + count) * UNIT)
                nc.sync.dma_start(out=out[:, cols].rearrange("(s p) j -> p s j", p=P), in_=staged)

        order = [(g, u) for g in range(GROUPS) for u in range(UNITS)]
        for step in range(len(order) + 3):
            if step < len(order):
                product(*order[step])
            if 0 <= step - 1 < UNITS:
                turn(step - 1)
            if step - 1 == 0:
                gather(1, HELD_PASS)
            if 0 <= step - 2 < UNITS:
                turn_back(step - 2)
            if 0 <= step - 2 < len(order):
                add_marks(*order[step - 2])
            if step in W5_AT:
                quantise_w5(W5_AT[step])
            if step >= 3:
                g, u = order[step - 3]
                if g == GROUPS - 1:
                    quantise(g, u, 1)
                    finish(u)
                elif u % PAIR == PAIR - 1:
                    quantise(g, u - PAIR + 1, PAIR)
